import numpy as np
import ml_dtypes


def mxq(x, axis, fmt="e4m3"):
    dtype, down = {"e4m3": (ml_dtypes.float8_e4m3fn, 7), "e5m2": (ml_dtypes.float8_e5m2, 14)}[fmt]
    v = np.moveaxis(np.asarray(x, np.float32).astype(ml_dtypes.bfloat16).astype(np.float64), axis, -1)
    blocks = v.reshape(v.shape[:-1] + (-1, 32))
    amax = np.abs(blocks).max(-1, keepdims=True)
    byte = np.maximum(np.where(amax > 0, np.frexp(amax)[1] - 1 + 127, 0) - down, 1)
    scale = np.exp2(byte - 127.0)
    codes = (blocks / scale).astype(np.float32).astype(dtype).astype(np.float64)
    return np.moveaxis((codes * scale).reshape(v.shape), -1, axis)


WIDE = False


def mx_kscale(k):
    if not WIDE:
        return np.ones(k)
    levels = np.array([10, -10, 5, -5, 0])
    if k % 512:
        return np.exp2(np.random.permutation(np.resize(levels, k // 32))).repeat(32)
    a = np.empty((k // 512, 16))
    for p in range(k // 512):
        a[p, :8] = np.random.permutation(np.resize(levels, 8))
        for g in range(8):
            far = levels[np.abs(levels - a[p, g]) >= 10]
            a[p, g + 8] = far[np.random.randint(len(far))]
    return np.exp2(a.ravel()).repeat(32)


def f64(x):
    return np.asarray(x).astype(np.float64)


def striped(idx):
    return np.tile(idx.reshape(-1, 16).T, (8, 1)).astype(np.uint16)


def unstriped(offs):
    return offs[:16].T.reshape(-1).astype(np.int64)


E2M1 = np.array([0.0, 0.5, 1.0, 1.5, 2.0, 3.0, 4.0, 6.0, -0.0, -0.5, -1.0, -1.5, -2.0, -3.0, -4.0, -6.0])


def pack_weight(w, fmt):
    k, n = w.shape
    w = f64(np.asarray(w, np.float32).astype(ml_dtypes.bfloat16)).reshape(k // 32, 32, n)
    amax = np.abs(w).max(1)
    if fmt == "e4m3":
        byte = np.frexp(amax)[1] - 1 + 127 - 7
    else:
        mant, ex = np.frexp(amax / 6.0)
        byte = np.where(mant > 0.5, ex, ex - 1) + 127
    byte = np.clip(np.where(amax > 0, byte, 1), 1, 254)
    scaled = (w * np.exp2(127.0 - byte)[:, None, :]).reshape(k, n).astype(np.float32)
    by_word = np.ascontiguousarray(scaled.reshape(k // 512, 128, 4, n).transpose(0, 1, 3, 2))
    if fmt == "e4m3":
        words = by_word.astype(ml_dtypes.float8_e4m3fn).view(np.uint8)
    else:
        c = by_word.astype(ml_dtypes.float4_e2m1fn).view(np.uint8) & 0xF
        words = (c[..., 0::2] | (c[..., 1::2] << 4)).reshape(k // 512, 128, 2 * n)
    return np.ascontiguousarray(words), np.ascontiguousarray(byte.astype(np.uint8).reshape(k // 512, 16, n))


def unpack_weight(words, scales, fmt):
    g, _, n = scales.shape
    words = np.ascontiguousarray(words).reshape(g, 128, n, -1)
    if fmt == "e4m3":
        vals = words.view(ml_dtypes.float8_e4m3fn).astype(np.float64)
    else:
        nib = np.empty((g, 128, n, 4), np.uint8)
        nib[..., 0::2] = words & 0xF
        nib[..., 1::2] = words >> 4
        vals = E2M1[nib]
    vals = vals * np.repeat(np.exp2(scales.astype(np.float64) - 127.0), 8, axis=1)[..., None]
    return vals.transpose(0, 1, 3, 2).reshape(g * 512, n)


def relu2(v):
    return np.maximum(v, 0.0) ** 2


K, T, E, C, H, N = 1024, 1280, 12, 128, 512, 128
TOP = 4
PAD = 64


def by_expert(wq, xq):
    return np.concatenate([wq[e].T @ xq[:, e * C:(e + 1) * C] for e in range(E)], axis=1)


def setup_inputs():
    n = np.random.standard_normal
    s = mx_kscale(K)[:, None]
    u = mx_kscale(H)
    slot_token = np.empty(E * C, np.int64); pos = np.tile(E * C + np.arange(T) % PAD, (TOP, 1)); taken = np.zeros(T, np.int64)
    liked = np.random.randn(T)
    for e in np.random.permutation(E):
        free = np.flatnonzero(taken < TOP); pick = np.random.permutation(free[np.argsort(-(liked[free] + np.random.gumbel(size=free.size)))[:C]]); slot_token[e * C:(e + 1) * C] = pick
        pos[taken[pick], pick] = e * C + np.arange(C); taken[pick] += 1
    g = np.random.uniform(0.2, 0.8, (TOP, T))
    x = pack_weight(n((K, T)) * s, "e4m3")
    return {
        "x_words": x[0],
        "x_scales": x[1],
        "w1": (n((E, K, H)) / np.sqrt(K) / s[None] * u[None, None, :]).astype(np.float32),
        "w2": (n((E, H, N)) / np.sqrt(H) / u[None, :, None] ** 2).astype(np.float32),
        "gate": np.stack([np.tile(r, (N, 1)) for r in g]).astype(np.float32),
        "offs": striped(slot_token),
        "pos1": striped(pos[0]),
        "pos2": striped(pos[1]),
        "pos3": striped(pos[2]),
        "pos4": striped(pos[3]),
    }


def reference(x_words, x_scales, w1, w2, gate, offs, pos1, pos2, pos3, pos4):
    idx = unstriped(offs)
    xq = unpack_weight(x_words, x_scales, "e4m3")[:, idx]
    h = relu2(by_expert(mxq(f64(w1), 1, "e4m3"), xq))
    y = by_expert(mxq(f64(w2), 1, "e4m3"), mxq(h, 0, "e4m3"))
    y = np.concatenate([y, np.zeros((N, PAD))], axis=1)
    return sum(f64(gate[r]) * y[:, unstriped(p)] for r, p in enumerate((pos1, pos2, pos3, pos4)))

@@ -1,0 +1,217 @@
+from contextlib import ExitStack
+
+import concourse.mybir as mybir
+from concourse.masks import make_identity
+
+K, T, E, C, H, N = 1024, 1280, 12, 128, 512, 128
+TOP, PAD = 4, 64
+SLOTS = E * C
+FLOPS = 2 * SLOTS * (K * H + H * N)
+
+F32 = mybir.dt.float32
+BF16 = mybir.dt.bfloat16
+I32 = mybir.dt.int32
+U32 = mybir.dt.uint32
+U16 = mybir.dt.uint16
+U8 = mybir.dt.uint8
+FP8X4 = mybir.dt.float8_e4m3fn_x4
+ACT = mybir.ActivationFunctionType
+
+P = 128
+PASSES = K // 512
+PIECE = 512
+CHUNK = 256
+BLOCKS = T // P
+W2_GROUPS = ((0, 1, 2, 3), (4, 5, 6, 7), (8, 9), (10, 11))
+
+
+def tile_moe_ecr_mlp_relu2_kernel(
+    tc, x_words, x_scales, w1, w2, gate, offs, pos1, pos2, pos3, pos4, out
+):
+    nc = tc.nc
+    with ExitStack() as ctx:
+        lists = ctx.enter_context(tc.tile_pool(name="lists", bufs=1))
+        keep = ctx.enter_context(tc.tile_pool(name="keep", bufs=1))
+        raws = ctx.enter_context(tc.tile_pool(name="raws", bufs=6))
+        work = ctx.enter_context(tc.tile_pool(name="work", bufs=4))
+        psum = ctx.enter_context(tc.psum_pool(name="psum", bufs=4))
+
+        offs_sb = lists.tile([P, SLOTS // 16], U16, name="offs_sb")
+        nc.sync.dma_start(offs_sb[:], offs)
+
+        token_scales = keep.tile([P, T], U8, name="token_scales", align_bytes=64)
+        nc.vector.memset(token_scales[:].bitcast(I32), 0)
+        gate_rows = keep.tile([P, P], F32, name="gate_rows")
+        nc.vector.memset(gate_rows[:], 0.0)
+        y_all = keep.tile([P, SLOTS + PAD], F32, name="y_all")
+        nc.vector.memset(y_all[:, SLOTS:], 0.0)
+        ident = keep.tile([P, P], F32, name="ident")
+        make_identity(nc, ident[:])
+
+        token_words = []
+        for o in range(PASSES):
+            words = keep.tile([P, T], I32, name="token_words%d" % o, align_bytes=64)
+            nc.sync.dma_start(words[:], x_words[o].rearrange("p t r -> p (t r)").bitcast(I32))
+            token_words.append(words)
+        for q in range(4):
+            nc.scalar.dma_start(
+                token_scales[32 * q : 32 * q + 4 * PASSES, :].bitcast(I32),
+                x_scales[:, 4 * q : 4 * q + 4, :].bitcast(I32),
+            )
+        nc.scalar.dma_start(
+            gate_rows[: TOP * BLOCKS, :], gate[:, 0, :].rearrange("r (b t) -> r b t", t=P)
+        )
+        gate_psum = psum.tile([P, P], F32, name="gate_psum", tag="wide")
+        nc.tensor.transpose(gate_psum[:], gate_rows[:], ident[:])
+        gate_cols = keep.tile([P, TOP * BLOCKS], F32, name="gate_cols")
+        nc.scalar.copy(gate_cols[:], gate_psum[:, : TOP * BLOCKS])
+
+        slot_words, slot_scales = {}, {}
+
+        def gather_tokens(piece):
+            picks = offs_sb[:, piece * PIECE // 16 : (piece + 1) * PIECE // 16]
+            for o in range(PASSES):
+                words = keep.tile([P, PIECE], U32, name="slot_words%d_%d" % (piece, o), align_bytes=64)
+                nc.vector.tensor_copy(words[:], token_words[o][:].bitcast(U32).indirect(picks))
+                slot_words[piece, o] = words
+            scales = keep.tile([P, PIECE], U8, name="slot_scales%d" % piece, align_bytes=64)
+            nc.vector.tensor_copy(scales[:], token_scales[:].indirect(picks))
+            slot_scales[piece] = scales
+
+        def load_w1(e, first, count):
+            raw = raws.tile([P, count, 4, H], F32, name="raw", tag="raw")
+            nc.sync.dma_start(
+                raw[:].rearrange("p o j i -> p o (j i)"),
+                w1[e, 512 * first : 512 * (first + count), :].rearrange("(o p j) i -> p o (j i)", p=P, j=4),
+            )
+            return raw
+
+        def quantize_w1(raw, count):
+            source = raw[:].rearrange("p o j (m u v) -> p u o m j v", u=2, v=2)
+            halves = []
+            for u, copy in enumerate((nc.vector.tensor_copy, nc.scalar.copy)):
+                rounded = work.tile([P, count, 2, P, 4], BF16, name="w1_rounded%d" % u, align_bytes=64)
+                copy(rounded[:].rearrange("p o v m j -> p o m j v"), source[:, u])
+                codes = work.tile([P, count, 2, P], U32, name="w1_codes%d" % u, align_bytes=64)
+                scales = work.tile([P, count, 2, P], U8, name="w1_scales%d" % u, align_bytes=64)
+                nc.vector.quantize_mx(
+                    out=codes[:].rearrange("p o v m -> p (o v m)").bitcast(FP8X4),
+                    scales=scales[:].rearrange("p o v m -> p (o v m)"),
+                    in_=rounded[:].rearrange("p o v m j -> p (o v m j)"),
+                )
+                halves.append((codes, scales))
+            return [[(codes[:, o], scales[:, o]) for codes, scales in halves] for o in range(count)]
+
+        h_quantized = {}
+
+        def first_product(e, w1_quantized):
+            piece, first = divmod(e * C, PIECE)
+            slots = slice(first, first + C)
+            a = psum.tile([P, 4, C], F32, name="a", tag="narrow")
+            for t in range(4):
+                u, v = divmod(t, 2)
+                for o in range(PASSES):
+                    codes, scales = w1_quantized[o][u]
+                    nc.tensor.matmul_mx(
+                        out=a[:, t, :],
+                        lhsT=codes[:, v].bitcast(FP8X4),
+                        lhsT_scale=scales[:, v],
+                        rhs=slot_words[piece, o][:, slots].bitcast(FP8X4),
+                        rhs_scale=slot_scales[piece][4 * o :, slots],
+                        start=(o == 0),
+                        stop=(o == PASSES - 1),
+                    )
+            return a
+
+        def quantize_h(e, a, positive):
+            nc.scalar.activation(positive.rearrange("p (c t) -> p c t", t=4), a[:].rearrange("p t c -> p c t"), ACT.Relu)
+            h = work.tile([P, C * 4], BF16, name="h", align_bytes=64)
+            nc.scalar.activation(h[:], positive, ACT.Square)
+            codes = keep.tile([P, C], U32, name="h_codes%d" % e, align_bytes=64)
+            scales = keep.tile([P, C], U8, name="h_scales%d" % e, align_bytes=64)
+            nc.vector.quantize_mx(out=codes[:].bitcast(FP8X4), scales=scales[:], in_=h[:])
+            h_quantized[e] = (codes, scales)
+
+        def quantize_w2(experts, on_vector):
+            count = len(experts)
+            raw = raws.tile([P, count, 4, N], F32, name="raw", tag="raw")
+            nc.sync.dma_start(
+                raw[:].rearrange("p e j n -> p e (j n)"),
+                w2[experts[0] : experts[0] + count].rearrange("e (p j) n -> p e (j n)", j=4),
+            )
+            rounded = work.tile([P, count, N, 4], BF16, name="w2_rounded", align_bytes=64)
+            target = rounded[:].rearrange("p e (c v) j -> p e c j v", v=2)
+            source = raw[:].rearrange("p e j (c v) -> p e c j v", v=2)
+            if on_vector:
+                nc.vector.tensor_copy(target[:, :on_vector], source[:, :on_vector])
+            nc.scalar.copy(target[:, on_vector:], source[:, on_vector:])
+            codes = work.tile([P, count * N], U32, name="w2_codes", align_bytes=64)
+            scales = work.tile([P, count * N], U8, name="w2_scales", align_bytes=64)
+            nc.vector.quantize_mx(
+                out=codes[:].bitcast(FP8X4), scales=scales[:], in_=rounded[:].rearrange("p e n j -> p (e n j)")
+            )
+            return codes, scales
+
+        def second_layer(experts, codes, scales):
+            y = psum.tile([P, len(experts) * C], F32, name="y", tag="wide")
+            for place, e in enumerate(experts):
+                cols = slice(place * N, (place + 1) * N)
+                h_codes, h_scales = h_quantized[e]
+                nc.tensor.matmul_mx(
+                    out=y[:, place * C : (place + 1) * C],
+                    lhsT=codes[:, cols].bitcast(FP8X4),
+                    lhsT_scale=scales[:, cols],
+                    rhs=h_codes[:].bitcast(FP8X4),
+                    rhs_scale=h_scales[:],
+                    start=True,
+                    stop=True,
+                )
+            nc.scalar.copy(y_all[:, experts[0] * C : (experts[-1] + 1) * C], y[:])
+
+        pos_sb = []
+        products = {}
+        for e in range(E):
+            if e * C % PIECE == 0:
+                gather_tokens(e * C // PIECE)
+            if e in (0, E - 1):
+                loaded = [load_w1(e, o, 1) for o in range(PASSES)]
+                w1_quantized = [quantize_w1(raw, 1)[0] for raw in loaded]
+            else:
+                loaded = [load_w1(e, 0, PASSES)]
+                w1_quantized = quantize_w1(loaded[0], PASSES)
+            if e > 0:
+                quantize_h(e - 1, products[e - 1], loaded[0][:, 0, 0, :])
+            products[e] = first_product(e, w1_quantized)
+            if e == 1:
+                for r, pos in enumerate((pos1, pos2, pos3, pos4)):
+                    tile = lists.tile([P, T // 16], U16, name="pos_sb%d" % r)
+                    nc.sync.dma_start(tile[:], pos)
+                    pos_sb.append(tile)
+            if e == W2_GROUPS[0][-1] + 1:
+                second_layer(W2_GROUPS[0], *quantize_w2(W2_GROUPS[0], 0))
+        last_positive = keep.tile([P, H], F32, name="last_positive")
+        quantize_h(E - 1, products[E - 1], last_positive[:])
+        for experts in W2_GROUPS[1:]:
+            second_layer(experts, *quantize_w2(experts, len(experts) // 2))
+
+        per_chunk = CHUNK // P
+        for chunk in range(T // CHUNK):
+            sums = [psum.tile([P, P], F32, name="sums", tag="wide") for b in range(per_chunk)]
+            for r in range(TOP):
+                picked = work.tile([P, CHUNK], F32, name="picked")
+                picks = pos_sb[r][:, chunk * CHUNK // 16 : (chunk + 1) * CHUNK // 16]
+                nc.vector.tensor_copy(picked[:], y_all[:].indirect(picks))
+                turned = psum.tile([P, per_chunk, P], F32, name="turned", tag="narrow")
+                for b in range(per_chunk):
+                    nc.tensor.transpose(turned[:, b, :], picked[:, b * P : (b + 1) * P], ident[:])
+                for b in range(per_chunk):
+                    column = r * BLOCKS + chunk * per_chunk + b
+                    gated = work.tile([P, P], F32, name="gated")
+                    nc.scalar.activation(gated[:], turned[:, b, :], ACT.Copy, scale=gate_cols[:, column : column + 1])
+                    nc.tensor.matmul(
+                        sums[b][:], lhsT=gated[:], rhs=ident[:], is_transpose=True, start=(r == 0), stop=(r == TOP - 1)
+                    )
+            result = work.tile([P, CHUNK], F32, name="result")
+            for b in range(per_chunk):
+                nc.scalar.copy(result[:, b * P : (b + 1) * P], sums[b][:])
+            nc.sync.dma_start(out[:, chunk * CHUNK : (chunk + 1) * CHUNK], result[:])

@@ -20,9 +20,10 @@ ACT = mybir.ActivationFunctionType
 P = 128
 PASSES = K // 512
 PIECE = 512
-CHUNK = 256
+CHUNK_BLOCKS = 2
+VECTOR_HEAVY_FROM = 8
 BLOCKS = T // P
-W2_GROUPS = ((0, 1, 2, 3), (4, 5, 6, 7), (8, 9), (10, 11))
+W2_GROUPS = ((0, 1, 2, 3), (4, 5, 6, 7), (8, 9), (10,), (11,))
 
 
 def tile_moe_ecr_mlp_relu2_kernel(
@@ -34,6 +35,8 @@ def tile_moe_ecr_mlp_relu2_kernel(
         keep = ctx.enter_context(tc.tile_pool(name="keep", bufs=1))
         raws = ctx.enter_context(tc.tile_pool(name="raws", bufs=6))
         work = ctx.enter_context(tc.tile_pool(name="work", bufs=4))
+        terms = ctx.enter_context(tc.tile_pool(name="terms", bufs=8))
+        pairs = ctx.enter_context(tc.tile_pool(name="pairs", bufs=2))
         psum = ctx.enter_context(tc.psum_pool(name="psum", bufs=4))
 
         offs_sb = lists.tile([P, SLOTS // 16], U16, name="offs_sb")
@@ -86,12 +89,16 @@ def tile_moe_ecr_mlp_relu2_kernel(
             )
             return raw
 
-        def quantize_w1(raw, count):
+        def quantize_w1(raw, count, on_vector):
             source = raw[:].rearrange("p o j (m u v) -> p u o m j v", u=2, v=2)
             halves = []
-            for u, copy in enumerate((nc.vector.tensor_copy, nc.scalar.copy)):
+            for u, split in enumerate((count, on_vector)):
                 rounded = work.tile([P, count, 2, P, 4], BF16, name="w1_rounded%d" % u, align_bytes=64)
-                copy(rounded[:].rearrange("p o v m j -> p o m j v"), source[:, u])
+                target = rounded[:].rearrange("p o v m j -> p o m j v")
+                if split > 0:
+                    nc.vector.tensor_copy(target[:, :split], source[:, u, :split])
+                if split < count:
+                    nc.scalar.copy(target[:, split:], source[:, u, split:])
                 codes = work.tile([P, count, 2, P], U32, name="w1_codes%d" % u, align_bytes=64)
                 scales = work.tile([P, count, 2, P], U8, name="w1_scales%d" % u, align_bytes=64)
                 nc.vector.quantize_mx(
@@ -139,14 +146,15 @@ def tile_moe_ecr_mlp_relu2_kernel(
                 raw[:].rearrange("p e j n -> p e (j n)"),
                 w2[experts[0] : experts[0] + count].rearrange("e (p j) n -> p e (j n)", j=4),
             )
-            rounded = work.tile([P, count, N, 4], BF16, name="w2_rounded", align_bytes=64)
+            rounded = pairs.tile([P, count, N, 4], BF16, name="w2_rounded", align_bytes=64)
             target = rounded[:].rearrange("p e (c v) j -> p e c j v", v=2)
             source = raw[:].rearrange("p e j (c v) -> p e c j v", v=2)
             if on_vector:
                 nc.vector.tensor_copy(target[:, :on_vector], source[:, :on_vector])
-            nc.scalar.copy(target[:, on_vector:], source[:, on_vector:])
-            codes = work.tile([P, count * N], U32, name="w2_codes", align_bytes=64)
-            scales = work.tile([P, count * N], U8, name="w2_scales", align_bytes=64)
+            if on_vector < count:
+                nc.scalar.copy(target[:, on_vector:], source[:, on_vector:])
+            codes = pairs.tile([P, count * N], U32, name="w2_codes", align_bytes=64)
+            scales = pairs.tile([P, count * N], U8, name="w2_scales", align_bytes=64)
             nc.vector.quantize_mx(
                 out=codes[:].bitcast(FP8X4), scales=scales[:], in_=rounded[:].rearrange("p e n j -> p (e n j)")
             )
@@ -175,10 +183,10 @@ def tile_moe_ecr_mlp_relu2_kernel(
                 gather_tokens(e * C // PIECE)
             if e in (0, E - 1):
                 loaded = [load_w1(e, o, 1) for o in range(PASSES)]
-                w1_quantized = [quantize_w1(raw, 1)[0] for raw in loaded]
+                w1_quantized = [quantize_w1(raw, 1, 0)[0] for raw in loaded]
             else:
                 loaded = [load_w1(e, 0, PASSES)]
-                w1_quantized = quantize_w1(loaded[0], PASSES)
+                w1_quantized = quantize_w1(loaded[0], PASSES, 1 if e >= VECTOR_HEAVY_FROM else 0)
             if e > 0:
                 quantize_h(e - 1, products[e - 1], loaded[0][:, 0, 0, :])
             products[e] = first_product(e, w1_quantized)
@@ -190,28 +198,39 @@ def tile_moe_ecr_mlp_relu2_kernel(
             if e == W2_GROUPS[0][-1] + 1:
                 second_layer(W2_GROUPS[0], *quantize_w2(W2_GROUPS[0], 0))
         last_positive = keep.tile([P, H], F32, name="last_positive")
+        for experts in W2_GROUPS[1:-1]:
+            second_layer(experts, *quantize_w2(experts, len(experts)))
+        last_w2 = quantize_w2(W2_GROUPS[-1], len(W2_GROUPS[-1]))
         quantize_h(E - 1, products[E - 1], last_positive[:])
-        for experts in W2_GROUPS[1:]:
-            second_layer(experts, *quantize_w2(experts, len(experts) // 2))
+        second_layer(W2_GROUPS[-1], *last_w2)
 
-        per_chunk = CHUNK // P
-        for chunk in range(T // CHUNK):
-            sums = [psum.tile([P, P], F32, name="sums", tag="wide") for b in range(per_chunk)]
+        for first in range(0, BLOCKS, CHUNK_BLOCKS):
+            tokens = slice(first * P, (first + CHUNK_BLOCKS) * P)
+            sums = [psum.tile([P, P], F32, name="sums", tag="wide") for b in range(CHUNK_BLOCKS)]
             for r in range(TOP):
-                picked = work.tile([P, CHUNK], F32, name="picked")
-                picks = pos_sb[r][:, chunk * CHUNK // 16 : (chunk + 1) * CHUNK // 16]
-                nc.vector.tensor_copy(picked[:], y_all[:].indirect(picks))
-                turned = psum.tile([P, per_chunk, P], F32, name="turned", tag="narrow")
-                for b in range(per_chunk):
-                    nc.tensor.transpose(turned[:, b, :], picked[:, b * P : (b + 1) * P], ident[:])
-                for b in range(per_chunk):
-                    column = r * BLOCKS + chunk * per_chunk + b
-                    gated = work.tile([P, P], F32, name="gated")
-                    nc.scalar.activation(gated[:], turned[:, b, :], ACT.Copy, scale=gate_cols[:, column : column + 1])
+                very_last = first + CHUNK_BLOCKS == BLOCKS and r == TOP - 1
+                picked = work.tile([P, CHUNK_BLOCKS * P], F32, name="picked")
+                nc.vector.tensor_copy(picked[:], y_all[:].indirect(pos_sb[r][:, tokens.start // 16 : tokens.stop // 16]))
+                if very_last:
+                    turned = [psum.tile([P, P], F32, name="turned", tag="narrow")[:] for b in range(CHUNK_BLOCKS)]
+                else:
+                    bank = psum.tile([P, CHUNK_BLOCKS, P], F32, name="turned", tag="narrow")
+                    turned = [bank[:, b, :] for b in range(CHUNK_BLOCKS)]
+                for b in range(CHUNK_BLOCKS):
+                    nc.tensor.transpose(turned[b], picked[:, b * P : (b + 1) * P], ident[:])
+                for b in range(CHUNK_BLOCKS):
+                    column = r * BLOCKS + first + b
+                    weight = gate_cols[:, column : column + 1]
+                    gated = terms.tile([P, P], F32, name="gated")
+                    if very_last and b == 1:
+                        nc.vector.tensor_scalar_mul(gated[:], turned[b], weight)
+                    else:
+                        nc.scalar.activation(gated[:], turned[b], ACT.Copy, scale=weight)
                     nc.tensor.matmul(
                         sums[b][:], lhsT=gated[:], rhs=ident[:], is_transpose=True, start=(r == 0), stop=(r == TOP - 1)
                     )
-            result = work.tile([P, CHUNK], F32, name="result")
-            for b in range(per_chunk):
-                nc.scalar.copy(result[:, b * P : (b + 1) * P], sums[b][:])
-            nc.sync.dma_start(out[:, chunk * CHUNK : (chunk + 1) * CHUNK], result[:])
+            result = pairs.tile([P, CHUNK_BLOCKS * P], F32, name="result")
+            for b in range(CHUNK_BLOCKS):
+                copy = nc.vector.tensor_copy if very_last and b == 1 else nc.scalar.copy
+                copy(result[:, b * P : (b + 1) * P], sums[b][:])
+            nc.sync.dma_start(out[:, tokens], result[:])

@@ -15,13 +15,14 @@ U32 = mybir.dt.uint32
 U16 = mybir.dt.uint16
 U8 = mybir.dt.uint8
 FP8X4 = mybir.dt.float8_e4m3fn_x4
+ALU = mybir.AluOpType
 ACT = mybir.ActivationFunctionType
 
 P = 128
 PASSES = K // 512
 PIECE = 512
 CHUNK_BLOCKS = 2
-VECTOR_HEAVY_FROM = 8
+DIRECT_BLOCKS = 4
 BLOCKS = T // P
 W2_GROUPS = ((0, 1, 2, 3), (4, 5, 6, 7), (8, 9), (10,), (11,))
 
@@ -36,7 +37,7 @@ def tile_moe_ecr_mlp_relu2_kernel(
         raws = ctx.enter_context(tc.tile_pool(name="raws", bufs=6))
         work = ctx.enter_context(tc.tile_pool(name="work", bufs=4))
         terms = ctx.enter_context(tc.tile_pool(name="terms", bufs=8))
-        pairs = ctx.enter_context(tc.tile_pool(name="pairs", bufs=2))
+        pairs = ctx.enter_context(tc.tile_pool(name="pairs", bufs=3))
         psum = ctx.enter_context(tc.psum_pool(name="psum", bufs=4))
 
         offs_sb = lists.tile([P, SLOTS // 16], U16, name="offs_sb")
@@ -181,12 +182,12 @@ def tile_moe_ecr_mlp_relu2_kernel(
         for e in range(E):
             if e * C % PIECE == 0:
                 gather_tokens(e * C // PIECE)
-            if e in (0, E - 1):
+            if e in (0, E - 2, E - 1):
                 loaded = [load_w1(e, o, 1) for o in range(PASSES)]
-                w1_quantized = [quantize_w1(raw, 1, 0)[0] for raw in loaded]
+                w1_quantized = [quantize_w1(raw, 1, int((e, o) == (E - 1, PASSES - 1)))[0] for o, raw in enumerate(loaded)]
             else:
                 loaded = [load_w1(e, 0, PASSES)]
-                w1_quantized = quantize_w1(loaded[0], PASSES, 1 if e >= VECTOR_HEAVY_FROM else 0)
+                w1_quantized = quantize_w1(loaded[0], PASSES, 0)
             if e > 0:
                 quantize_h(e - 1, products[e - 1], loaded[0][:, 0, 0, :])
             products[e] = first_product(e, w1_quantized)
@@ -198,39 +199,56 @@ def tile_moe_ecr_mlp_relu2_kernel(
             if e == W2_GROUPS[0][-1] + 1:
                 second_layer(W2_GROUPS[0], *quantize_w2(W2_GROUPS[0], 0))
         last_positive = keep.tile([P, H], F32, name="last_positive")
-        for experts in W2_GROUPS[1:-1]:
-            second_layer(experts, *quantize_w2(experts, len(experts)))
+        second_layer(W2_GROUPS[1], *quantize_w2(W2_GROUPS[1], 3))
+        for experts in W2_GROUPS[2:-1]:
+            second_layer(experts, *quantize_w2(experts, len(experts) // 2 * 2))
         last_w2 = quantize_w2(W2_GROUPS[-1], len(W2_GROUPS[-1]))
         quantize_h(E - 1, products[E - 1], last_positive[:])
         second_layer(W2_GROUPS[-1], *last_w2)
 
+        direct_first = BLOCKS - DIRECT_BLOCKS
+        last_gate = raws.tile([P, DIRECT_BLOCKS * P], F32, name="raw", tag="raw")
+        nc.sync.dma_start(last_gate[:], gate[TOP - 1, :, direct_first * P :])
+
+        def picks(r, first):
+            return pos_sb[r][:, first * P // 16 : (first + CHUNK_BLOCKS) * P // 16]
+
+        sums = {}
         for first in range(0, BLOCKS, CHUNK_BLOCKS):
-            tokens = slice(first * P, (first + CHUNK_BLOCKS) * P)
-            sums = [psum.tile([P, P], F32, name="sums", tag="wide") for b in range(CHUNK_BLOCKS)]
-            for r in range(TOP):
-                very_last = first + CHUNK_BLOCKS == BLOCKS and r == TOP - 1
+            turned_terms = TOP if first < direct_first else TOP - 1
+            for b in range(CHUNK_BLOCKS):
+                sums[first + b] = psum.tile([P, P], F32, name="sums", tag="wide")
+            for r in range(turned_terms):
                 picked = work.tile([P, CHUNK_BLOCKS * P], F32, name="picked")
-                nc.vector.tensor_copy(picked[:], y_all[:].indirect(pos_sb[r][:, tokens.start // 16 : tokens.stop // 16]))
-                if very_last:
-                    turned = [psum.tile([P, P], F32, name="turned", tag="narrow")[:] for b in range(CHUNK_BLOCKS)]
-                else:
-                    bank = psum.tile([P, CHUNK_BLOCKS, P], F32, name="turned", tag="narrow")
-                    turned = [bank[:, b, :] for b in range(CHUNK_BLOCKS)]
+                nc.vector.tensor_copy(picked[:], y_all[:].indirect(picks(r, first)))
+                turned = psum.tile([P, CHUNK_BLOCKS, P], F32, name="turned", tag="narrow")
                 for b in range(CHUNK_BLOCKS):
-                    nc.tensor.transpose(turned[b], picked[:, b * P : (b + 1) * P], ident[:])
+                    nc.tensor.transpose(turned[:, b, :], picked[:, b * P : (b + 1) * P], ident[:])
                 for b in range(CHUNK_BLOCKS):
                     column = r * BLOCKS + first + b
-                    weight = gate_cols[:, column : column + 1]
                     gated = terms.tile([P, P], F32, name="gated")
-                    if very_last and b == 1:
-                        nc.vector.tensor_scalar_mul(gated[:], turned[b], weight)
-                    else:
-                        nc.scalar.activation(gated[:], turned[b], ACT.Copy, scale=weight)
+                    nc.scalar.activation(gated[:], turned[:, b, :], ACT.Copy, scale=gate_cols[:, column : column + 1])
                     nc.tensor.matmul(
-                        sums[b][:], lhsT=gated[:], rhs=ident[:], is_transpose=True, start=(r == 0), stop=(r == TOP - 1)
+                        sums[first + b][:],
+                        lhsT=gated[:],
+                        rhs=ident[:],
+                        is_transpose=True,
+                        start=(r == 0),
+                        stop=(r == turned_terms - 1),
                     )
+            if first < direct_first:
+                result = pairs.tile([P, CHUNK_BLOCKS * P], F32, name="result")
+                for b in range(CHUNK_BLOCKS):
+                    nc.scalar.copy(result[:, b * P : (b + 1) * P], sums[first + b][:])
+                nc.sync.dma_start(out[:, first * P : (first + CHUNK_BLOCKS) * P], result[:])
+        last_terms = {}
+        for first in range(direct_first, BLOCKS, CHUNK_BLOCKS):
+            last_terms[first] = work.tile([P, CHUNK_BLOCKS * P], F32, name="picked")
+            weights = last_gate[:, (first - direct_first) * P : (first - direct_first + CHUNK_BLOCKS) * P]
+            nc.vector.tensor_tensor(last_terms[first][:], y_all[:].indirect(picks(TOP - 1, first)), weights, ALU.mult)
+        for first in range(direct_first, BLOCKS, CHUNK_BLOCKS):
             result = pairs.tile([P, CHUNK_BLOCKS * P], F32, name="result")
             for b in range(CHUNK_BLOCKS):
-                copy = nc.vector.tensor_copy if very_last and b == 1 else nc.scalar.copy
-                copy(result[:, b * P : (b + 1) * P], sums[b][:])
-            nc.sync.dma_start(out[:, tokens], result[:])
+                cols = slice(b * P, (b + 1) * P)
+                nc.vector.tensor_tensor(result[:, cols], sums[first + b][:], last_terms[first][:, cols], ALU.add)
+            nc.sync.dma_start(out[:, first * P : (first + CHUNK_BLOCKS) * P], result[:])

@@ -22,8 +22,7 @@ P = 128
 PASSES = K // 512
 PIECE = 512
 CHUNK_BLOCKS = 2
-DIRECT_BLOCKS = 4
-BLOCKS = T // P
+DIRECT_CHUNKS = 2
 W2_GROUPS = ((0, 1, 2, 3), (4, 5, 6, 7), (8, 9), (10,), (11,))
 
 
@@ -45,8 +44,6 @@ def tile_moe_ecr_mlp_relu2_kernel(
 
         token_scales = keep.tile([P, T], U8, name="token_scales", align_bytes=64)
         nc.vector.memset(token_scales[:].bitcast(I32), 0)
-        gate_rows = keep.tile([P, P], F32, name="gate_rows")
-        nc.vector.memset(gate_rows[:], 0.0)
         y_all = keep.tile([P, SLOTS + PAD], F32, name="y_all")
         nc.vector.memset(y_all[:, SLOTS:], 0.0)
         ident = keep.tile([P, P], F32, name="ident")
@@ -62,13 +59,6 @@ def tile_moe_ecr_mlp_relu2_kernel(
                 token_scales[32 * q : 32 * q + 4 * PASSES, :].bitcast(I32),
                 x_scales[:, 4 * q : 4 * q + 4, :].bitcast(I32),
             )
-        nc.scalar.dma_start(
-            gate_rows[: TOP * BLOCKS, :], gate[:, 0, :].rearrange("r (b t) -> r b t", t=P)
-        )
-        gate_psum = psum.tile([P, P], F32, name="gate_psum", tag="wide")
-        nc.tensor.transpose(gate_psum[:], gate_rows[:], ident[:])
-        gate_cols = keep.tile([P, TOP * BLOCKS], F32, name="gate_cols")
-        nc.scalar.copy(gate_cols[:], gate_psum[:, : TOP * BLOCKS])
 
         slot_words, slot_scales = {}, {}
 
@@ -206,49 +196,52 @@ def tile_moe_ecr_mlp_relu2_kernel(
         quantize_h(E - 1, products[E - 1], last_positive[:])
         second_layer(W2_GROUPS[-1], *last_w2)
 
-        direct_first = BLOCKS - DIRECT_BLOCKS
-        last_gate = raws.tile([P, DIRECT_BLOCKS * P], F32, name="raw", tag="raw")
-        nc.sync.dma_start(last_gate[:], gate[TOP - 1, :, direct_first * P :])
+        width = CHUNK_BLOCKS * P
+        chunks = T // width
+        gates = []
+        for chunk in range(chunks):
+            tile = raws.tile([P, TOP, width], F32, name="raw", tag="raw")
+            nc.sync.dma_start(tile[:], gate[:, :, chunk * width : (chunk + 1) * width].rearrange("r n t -> n r t"))
+            gates.append(tile)
 
-        def picks(r, first):
-            return pos_sb[r][:, first * P // 16 : (first + CHUNK_BLOCKS) * P // 16]
+        def gated_term(r, chunk):
+            term = terms.tile([P, width], F32, name="term")
+            picks = pos_sb[r][:, chunk * width // 16 : (chunk + 1) * width // 16]
+            nc.vector.tensor_tensor(term[:], y_all[:].indirect(picks), gates[chunk][:, r, :], ALU.mult)
+            return term
 
-        sums = {}
-        for first in range(0, BLOCKS, CHUNK_BLOCKS):
-            turned_terms = TOP if first < direct_first else TOP - 1
-            for b in range(CHUNK_BLOCKS):
-                sums[first + b] = psum.tile([P, P], F32, name="sums", tag="wide")
-            for r in range(turned_terms):
-                picked = work.tile([P, CHUNK_BLOCKS * P], F32, name="picked")
-                nc.vector.tensor_copy(picked[:], y_all[:].indirect(picks(r, first)))
-                turned = psum.tile([P, CHUNK_BLOCKS, P], F32, name="turned", tag="narrow")
+        def sum_terms(chunk, count):
+            turned = [psum.tile([P, P], F32, name="turned", tag="narrow") for b in range(CHUNK_BLOCKS)]
+            for r in range(count):
+                term = gated_term(r, chunk)
                 for b in range(CHUNK_BLOCKS):
-                    nc.tensor.transpose(turned[:, b, :], picked[:, b * P : (b + 1) * P], ident[:])
-                for b in range(CHUNK_BLOCKS):
-                    column = r * BLOCKS + first + b
-                    gated = terms.tile([P, P], F32, name="gated")
-                    nc.scalar.activation(gated[:], turned[:, b, :], ACT.Copy, scale=gate_cols[:, column : column + 1])
                     nc.tensor.matmul(
-                        sums[first + b][:],
-                        lhsT=gated[:],
+                        turned[b][:],
+                        lhsT=term[:, b * P : (b + 1) * P],
                         rhs=ident[:],
                         is_transpose=True,
                         start=(r == 0),
-                        stop=(r == turned_terms - 1),
+                        stop=(r == count - 1),
                     )
-            if first < direct_first:
-                result = pairs.tile([P, CHUNK_BLOCKS * P], F32, name="result")
-                for b in range(CHUNK_BLOCKS):
-                    nc.scalar.copy(result[:, b * P : (b + 1) * P], sums[first + b][:])
-                nc.sync.dma_start(out[:, first * P : (first + CHUNK_BLOCKS) * P], result[:])
-        last_terms = {}
-        for first in range(direct_first, BLOCKS, CHUNK_BLOCKS):
-            last_terms[first] = work.tile([P, CHUNK_BLOCKS * P], F32, name="picked")
-            weights = last_gate[:, (first - direct_first) * P : (first - direct_first + CHUNK_BLOCKS) * P]
-            nc.vector.tensor_tensor(last_terms[first][:], y_all[:].indirect(picks(TOP - 1, first)), weights, ALU.mult)
-        for first in range(direct_first, BLOCKS, CHUNK_BLOCKS):
-            result = pairs.tile([P, CHUNK_BLOCKS * P], F32, name="result")
+            sums = psum.tile([P, width], F32, name="sums", tag="wide")
             for b in range(CHUNK_BLOCKS):
-                cols = slice(b * P, (b + 1) * P)
-                nc.vector.tensor_tensor(result[:, cols], sums[first + b][:], last_terms[first][:, cols], ALU.add)
-            nc.sync.dma_start(out[:, first * P : (first + CHUNK_BLOCKS) * P], result[:])
+                staged = work.tile([P, P], F32, name="staged")
+                nc.scalar.copy(staged[:], turned[b][:])
+                nc.tensor.transpose(sums[:, b * P : (b + 1) * P], staged[:], ident[:])
+            return sums
+
+        def store(chunk, result):
+            nc.sync.dma_start(out[:, chunk * width : (chunk + 1) * width], result[:])
+
+        for chunk in range(chunks - DIRECT_CHUNKS):
+            sums = sum_terms(chunk, TOP)
+            result = pairs.tile([P, width], F32, name="result")
+            nc.scalar.copy(result[:], sums[:])
+            store(chunk, result)
+        closing = range(chunks - DIRECT_CHUNKS, chunks)
+        partial = [sum_terms(chunk, TOP - 1) for chunk in closing]
+        last_terms = [gated_term(TOP - 1, chunk) for chunk in closing]
+        for chunk, sums, term in zip(closing, partial, last_terms):
+            result = pairs.tile([P, width], F32, name="result")
+            nc.vector.tensor_tensor(result[:], sums[:], term[:], ALU.add)
+            store(chunk, result)

@@ -22,7 +22,7 @@ P = 128
 PASSES = K // 512
 PIECE = 512
 CHUNK_BLOCKS = 2
-DIRECT_CHUNKS = 2
+DIRECT_CHUNKS = 3
 W2_GROUPS = ((0, 1, 2, 3), (4, 5, 6, 7), (8, 9), (10,), (11,))
 
 
@@ -39,9 +39,6 @@ def tile_moe_ecr_mlp_relu2_kernel(
         pairs = ctx.enter_context(tc.tile_pool(name="pairs", bufs=3))
         psum = ctx.enter_context(tc.psum_pool(name="psum", bufs=4))
 
-        offs_sb = lists.tile([P, SLOTS // 16], U16, name="offs_sb")
-        nc.sync.dma_start(offs_sb[:], offs)
-
         token_scales = keep.tile([P, T], U8, name="token_scales", align_bytes=64)
         nc.vector.memset(token_scales[:].bitcast(I32), 0)
         y_all = keep.tile([P, SLOTS + PAD], F32, name="y_all")
@@ -54,6 +51,9 @@ def tile_moe_ecr_mlp_relu2_kernel(
             words = keep.tile([P, T], I32, name="token_words%d" % o, align_bytes=64)
             nc.sync.dma_start(words[:], x_words[o].rearrange("p t r -> p (t r)").bitcast(I32))
             token_words.append(words)
+            if o == 0:
+                offs_sb = lists.tile([P, SLOTS // 16], U16, name="offs_sb")
+                nc.sync.dma_start(offs_sb[:], offs)
         for q in range(4):
             nc.scalar.dma_start(
                 token_scales[32 * q : 32 * q + 4 * PASSES, :].bitcast(I32),
@@ -130,7 +130,7 @@ def tile_moe_ecr_mlp_relu2_kernel(
             nc.vector.quantize_mx(out=codes[:].bitcast(FP8X4), scales=scales[:], in_=h[:])
             h_quantized[e] = (codes, scales)
 
-        def quantize_w2(experts, on_vector):
+        def quantize_w2(experts, on_vector, parts=1):
             count = len(experts)
             raw = raws.tile([P, count, 4, N], F32, name="raw", tag="raw")
             nc.sync.dma_start(
@@ -140,15 +140,22 @@ def tile_moe_ecr_mlp_relu2_kernel(
             rounded = pairs.tile([P, count, N, 4], BF16, name="w2_rounded", align_bytes=64)
             target = rounded[:].rearrange("p e (c v) j -> p e c j v", v=2)
             source = raw[:].rearrange("p e j (c v) -> p e c j v", v=2)
+            step = N // 2 // parts
             if on_vector:
-                nc.vector.tensor_copy(target[:, :on_vector], source[:, :on_vector])
+                for part in range(parts):
+                    cols = slice(part * step, (part + 1) * step)
+                    nc.vector.tensor_copy(target[:, :on_vector, cols], source[:, :on_vector, cols])
             if on_vector < count:
                 nc.scalar.copy(target[:, on_vector:], source[:, on_vector:])
             codes = pairs.tile([P, count * N], U32, name="w2_codes", align_bytes=64)
             scales = pairs.tile([P, count * N], U8, name="w2_scales", align_bytes=64)
-            nc.vector.quantize_mx(
-                out=codes[:].bitcast(FP8X4), scales=scales[:], in_=rounded[:].rearrange("p e n j -> p (e n j)")
-            )
+            values = rounded[:].rearrange("p e n j -> p (e n j)")
+            step = count * N // parts
+            for part in range(parts):
+                cols = slice(part * step, (part + 1) * step)
+                nc.vector.quantize_mx(
+                    out=codes[:, cols].bitcast(FP8X4), scales=scales[:, cols], in_=values[:, 4 * cols.start : 4 * cols.stop]
+                )
             return codes, scales
 
         def second_layer(experts, codes, scales):
@@ -192,7 +199,7 @@ def tile_moe_ecr_mlp_relu2_kernel(
         second_layer(W2_GROUPS[1], *quantize_w2(W2_GROUPS[1], 3))
         for experts in W2_GROUPS[2:-1]:
             second_layer(experts, *quantize_w2(experts, len(experts) // 2 * 2))
-        last_w2 = quantize_w2(W2_GROUPS[-1], len(W2_GROUPS[-1]))
+        last_w2 = quantize_w2(W2_GROUPS[-1], len(W2_GROUPS[-1]), 2)
         quantize_h(E - 1, products[E - 1], last_positive[:])
         second_layer(W2_GROUPS[-1], *last_w2)
 

@@ -21,9 +21,13 @@ ACT = mybir.ActivationFunctionType
 P = 128
 PASSES = K // 512
 PIECE = 512
-CHUNK_BLOCKS = 2
-DIRECT_CHUNKS = 3
-W2_GROUPS = ((0, 1, 2, 3), (4, 5, 6, 7), (8, 9), (10,), (11,))
+OPENING = 512
+CHUNK = 256
+EARLY_W2 = {3: (0, 1, 2), 7: (3, 4, 5)}
+LATE_W2_LOADS = ((6,), (7, 8), (9,), (10,), (11,))
+LATE_Y = ((6, 7, 8), (9, 10), (11,))
+LAST_ON_VECTOR = 32
+SHARED_FROM = 9
 
 
 def tile_moe_ecr_mlp_relu2_kernel(
@@ -35,8 +39,9 @@ def tile_moe_ecr_mlp_relu2_kernel(
         keep = ctx.enter_context(tc.tile_pool(name="keep", bufs=1))
         raws = ctx.enter_context(tc.tile_pool(name="raws", bufs=6))
         work = ctx.enter_context(tc.tile_pool(name="work", bufs=4))
-        terms = ctx.enter_context(tc.tile_pool(name="terms", bufs=8))
-        pairs = ctx.enter_context(tc.tile_pool(name="pairs", bufs=3))
+        rounding = ctx.enter_context(tc.tile_pool(name="rounding", bufs=2))
+        late = ctx.enter_context(tc.tile_pool(name="late", bufs=1))
+        terms = ctx.enter_context(tc.tile_pool(name="terms", bufs=1))
         psum = ctx.enter_context(tc.psum_pool(name="psum", bufs=4))
 
         token_scales = keep.tile([P, T], U8, name="token_scales", align_bytes=64)
@@ -83,13 +88,16 @@ def tile_moe_ecr_mlp_relu2_kernel(
         def quantize_w1(raw, count, on_vector):
             source = raw[:].rearrange("p o j (m u v) -> p u o m j v", u=2, v=2)
             halves = []
-            for u, split in enumerate((count, on_vector)):
-                rounded = work.tile([P, count, 2, P, 4], BF16, name="w1_rounded%d" % u, align_bytes=64)
+            for u, split in enumerate((P, on_vector)):
+                rounded = rounding.tile([P, count, 2, P, 4], BF16, name="w1_rounded%d" % u, align_bytes=64)
                 target = rounded[:].rearrange("p o v m j -> p o m j v")
                 if split > 0:
-                    nc.vector.tensor_copy(target[:, :split], source[:, u, :split])
-                if split < count:
-                    nc.scalar.copy(target[:, split:], source[:, u, split:])
+                    nc.vector.tensor_copy(target[:, :, :split], source[:, u, :, :split])
+                if split < P:
+                    nc.scalar.copy(target[:, :, split:], source[:, u, :, split:])
+                halves.append(rounded)
+            quantized = []
+            for u, rounded in enumerate(halves):
                 codes = work.tile([P, count, 2, P], U32, name="w1_codes%d" % u, align_bytes=64)
                 scales = work.tile([P, count, 2, P], U8, name="w1_scales%d" % u, align_bytes=64)
                 nc.vector.quantize_mx(
@@ -97,8 +105,8 @@ def tile_moe_ecr_mlp_relu2_kernel(
                     scales=scales[:].rearrange("p o v m -> p (o v m)"),
                     in_=rounded[:].rearrange("p o v m j -> p (o v m j)"),
                 )
-                halves.append((codes, scales))
-            return [[(codes[:, o], scales[:, o]) for codes, scales in halves] for o in range(count)]
+                quantized.append((codes, scales))
+            return [[(codes[:, o], scales[:, o]) for codes, scales in quantized] for o in range(count)]
 
         h_quantized = {}
 
@@ -106,9 +114,9 @@ def tile_moe_ecr_mlp_relu2_kernel(
             piece, first = divmod(e * C, PIECE)
             slots = slice(first, first + C)
             a = psum.tile([P, 4, C], F32, name="a", tag="narrow")
-            for t in range(4):
-                u, v = divmod(t, 2)
-                for o in range(PASSES):
+            for o in range(PASSES):
+                for t in range(4):
+                    u, v = divmod(t, 2)
                     codes, scales = w1_quantized[o][u]
                     nc.tensor.matmul_mx(
                         out=a[:, t, :],
@@ -116,8 +124,8 @@ def tile_moe_ecr_mlp_relu2_kernel(
                         lhsT_scale=scales[:, v],
                         rhs=slot_words[piece, o][:, slots].bitcast(FP8X4),
                         rhs_scale=slot_scales[piece][4 * o :, slots],
-                        start=(o == 0),
-                        stop=(o == PASSES - 1),
+                        start=(o, t) == (0, 0),
+                        stop=(o, t) == (PASSES - 1, 3),
                     )
             return a
 
@@ -130,43 +138,42 @@ def tile_moe_ecr_mlp_relu2_kernel(
             nc.vector.quantize_mx(out=codes[:].bitcast(FP8X4), scales=scales[:], in_=h[:])
             h_quantized[e] = (codes, scales)
 
-        def quantize_w2(experts, on_vector, parts=1):
-            count = len(experts)
-            raw = raws.tile([P, count, 4, N], F32, name="raw", tag="raw")
+        w2_quantized = {}
+
+        def load_w2(experts):
+            raw = raws.tile([P, len(experts), 4, N], F32, name="raw", tag="raw")
             nc.sync.dma_start(
                 raw[:].rearrange("p e j n -> p e (j n)"),
-                w2[experts[0] : experts[0] + count].rearrange("e (p j) n -> p e (j n)", j=4),
+                w2[experts[0] : experts[-1] + 1].rearrange("e (p j) n -> p e (j n)", j=4),
             )
-            rounded = pairs.tile([P, count, N, 4], BF16, name="w2_rounded", align_bytes=64)
-            target = rounded[:].rearrange("p e (c v) j -> p e c j v", v=2)
-            source = raw[:].rearrange("p e j (c v) -> p e c j v", v=2)
-            step = N // 2 // parts
-            if on_vector:
-                for part in range(parts):
-                    cols = slice(part * step, (part + 1) * step)
-                    nc.vector.tensor_copy(target[:, :on_vector, cols], source[:, :on_vector, cols])
-            if on_vector < count:
-                nc.scalar.copy(target[:, on_vector:], source[:, on_vector:])
-            codes = pairs.tile([P, count * N], U32, name="w2_codes", align_bytes=64)
-            scales = pairs.tile([P, count * N], U8, name="w2_scales", align_bytes=64)
-            values = rounded[:].rearrange("p e n j -> p (e n j)")
-            step = count * N // parts
-            for part in range(parts):
-                cols = slice(part * step, (part + 1) * step)
-                nc.vector.quantize_mx(
-                    out=codes[:, cols].bitcast(FP8X4), scales=scales[:, cols], in_=values[:, 4 * cols.start : 4 * cols.stop]
-                )
-            return codes, scales
+            return raw
 
-        def second_layer(experts, codes, scales):
+        def quantize_w2(experts, raw, pool, suffix, on_scalar=False):
+            count = len(experts)
+            rounded = pool.tile([P, count, N, 4], BF16, name="w2_rounded" + suffix, align_bytes=64)
+            target = rounded[:].rearrange("p e (c v) j -> p e c j v", v=4)
+            source = raw[:].rearrange("p e j (c v) -> p e c j v", v=4)
+            values = rounded[:].rearrange("p e n j -> p e (n j)")
+            codes = pool.tile([P, count, N], U32, name="w2_codes" + suffix, align_bytes=64)
+            scales = pool.tile([P, count, N], U8, name="w2_scales" + suffix, align_bytes=64)
+            for place, e in enumerate(experts):
+                if on_scalar:
+                    nc.scalar.copy(target[:, place], source[:, place])
+                else:
+                    nc.vector.tensor_copy(target[:, place], source[:, place])
+            for place, e in enumerate(experts):
+                nc.vector.quantize_mx(out=codes[:, place].bitcast(FP8X4), scales=scales[:, place], in_=values[:, place])
+                w2_quantized[e] = (codes[:, place], scales[:, place])
+
+        def second_layer(experts):
             y = psum.tile([P, len(experts) * C], F32, name="y", tag="wide")
             for place, e in enumerate(experts):
-                cols = slice(place * N, (place + 1) * N)
+                codes, scales = w2_quantized[e]
                 h_codes, h_scales = h_quantized[e]
                 nc.tensor.matmul_mx(
                     out=y[:, place * C : (place + 1) * C],
-                    lhsT=codes[:, cols].bitcast(FP8X4),
-                    lhsT_scale=scales[:, cols],
+                    lhsT=codes.bitcast(FP8X4),
+                    lhsT_scale=scales,
                     rhs=h_codes[:].bitcast(FP8X4),
                     rhs_scale=h_scales[:],
                     start=True,
@@ -179,12 +186,15 @@ def tile_moe_ecr_mlp_relu2_kernel(
         for e in range(E):
             if e * C % PIECE == 0:
                 gather_tokens(e * C // PIECE)
+            share = LAST_ON_VECTOR if e >= SHARED_FROM else 0
             if e in (0, E - 2, E - 1):
                 loaded = [load_w1(e, o, 1) for o in range(PASSES)]
-                w1_quantized = [quantize_w1(raw, 1, int((e, o) == (E - 1, PASSES - 1)))[0] for o, raw in enumerate(loaded)]
+                w1_quantized = [
+                    quantize_w1(raw, 1, share)[0] for raw in loaded
+                ]
             else:
                 loaded = [load_w1(e, 0, PASSES)]
-                w1_quantized = quantize_w1(loaded[0], PASSES, 0)
+                w1_quantized = quantize_w1(loaded[0], PASSES, share)
             if e > 0:
                 quantize_h(e - 1, products[e - 1], loaded[0][:, 0, 0, :])
             products[e] = first_product(e, w1_quantized)
@@ -193,62 +203,81 @@ def tile_moe_ecr_mlp_relu2_kernel(
                     tile = lists.tile([P, T // 16], U16, name="pos_sb%d" % r)
                     nc.sync.dma_start(tile[:], pos)
                     pos_sb.append(tile)
-            if e == W2_GROUPS[0][-1] + 1:
-                second_layer(W2_GROUPS[0], *quantize_w2(W2_GROUPS[0], 0))
+            if e in EARLY_W2:
+                quantize_w2(EARLY_W2[e], load_w2(EARLY_W2[e]), late, "_early")
+                second_layer(EARLY_W2[e])
         last_positive = keep.tile([P, H], F32, name="last_positive")
-        second_layer(W2_GROUPS[1], *quantize_w2(W2_GROUPS[1], 3))
-        for experts in W2_GROUPS[2:-1]:
-            second_layer(experts, *quantize_w2(experts, len(experts) // 2 * 2))
-        last_w2 = quantize_w2(W2_GROUPS[-1], len(W2_GROUPS[-1]), 2)
         quantize_h(E - 1, products[E - 1], last_positive[:])
-        second_layer(W2_GROUPS[-1], *last_w2)
+        for experts in LATE_W2_LOADS:
+            raw = load_w2(experts)
+            quantize_w2(experts, raw, late, "_%d" % experts[0], on_scalar=experts == LATE_W2_LOADS[0])
+        for experts in LATE_Y:
+            second_layer(experts)
 
-        width = CHUNK_BLOCKS * P
-        chunks = T // width
-        gates = []
-        for chunk in range(chunks):
-            tile = raws.tile([P, TOP, width], F32, name="raw", tag="raw")
-            nc.sync.dma_start(tile[:], gate[:, :, chunk * width : (chunk + 1) * width].rearrange("r n t -> n r t"))
-            gates.append(tile)
+        def load_gate(ranks, tokens):
+            tile = raws.tile([P, len(ranks), len(tokens)], F32, name="raw", tag="raw")
+            nc.sync.dma_start(
+                tile[:], gate[ranks.start : ranks.stop, :, tokens.start : tokens.stop].rearrange("r n t -> n r t")
+            )
+            for place, r in enumerate(ranks):
+                gates[r, tokens.start >= OPENING] = tile[:, place, :]
 
-        def gated_term(r, chunk):
-            term = terms.tile([P, width], F32, name="term")
-            picks = pos_sb[r][:, chunk * width // 16 : (chunk + 1) * width // 16]
-            nc.vector.tensor_tensor(term[:], y_all[:].indirect(picks), gates[chunk][:, r, :], ALU.mult)
+        opening, closing = range(0, OPENING), range(OPENING, T)
+        gates = {}
+        load_gate(range(3, 4), opening)
+        load_gate(range(0, 3), opening)
+        load_gate(range(2, 4), closing)
+        load_gate(range(0, 2), closing)
+
+        def gated_term(r, tokens):
+            term = terms.tile([P, len(tokens)], F32, name="term%d_%d" % (r, tokens.start))
+            picks = pos_sb[r][:, tokens.start // 16 : tokens.stop // 16]
+            first = OPENING if tokens.start >= OPENING else 0
+            factor = gates[r, tokens.start >= OPENING][:, tokens.start - first : tokens.stop - first]
+            nc.vector.tensor_tensor(term[:], y_all[:].indirect(picks), factor, ALU.mult)
             return term
 
-        def sum_terms(chunk, count):
-            turned = [psum.tile([P, P], F32, name="turned", tag="narrow") for b in range(CHUNK_BLOCKS)]
-            for r in range(count):
-                term = gated_term(r, chunk)
-                for b in range(CHUNK_BLOCKS):
-                    nc.tensor.matmul(
-                        turned[b][:],
-                        lhsT=term[:, b * P : (b + 1) * P],
-                        rhs=ident[:],
-                        is_transpose=True,
-                        start=(r == 0),
-                        stop=(r == count - 1),
-                    )
+        def add_turned(turned, term, start, stop):
+            blocks = turned.shape[1] // P
+            for b in range(blocks):
+                nc.tensor.matmul(
+                    turned[:, b * P : (b + 1) * P],
+                    lhsT=term[:, b * P : (b + 1) * P],
+                    rhs=ident[:],
+                    is_transpose=True,
+                    start=start and b == 0,
+                    stop=stop and b == blocks - 1,
+                )
+
+        def turn_back(turned, name):
+            width = turned.shape[1]
+            staged = terms.tile([P, width], F32, name="staged" + name)
+            nc.scalar.copy(staged[:], turned[:])
             sums = psum.tile([P, width], F32, name="sums", tag="wide")
-            for b in range(CHUNK_BLOCKS):
-                staged = work.tile([P, P], F32, name="staged")
-                nc.scalar.copy(staged[:], turned[b][:])
-                nc.tensor.transpose(sums[:, b * P : (b + 1) * P], staged[:], ident[:])
+            for b in range(width // P):
+                nc.tensor.transpose(sums[:, b * P : (b + 1) * P], staged[:, b * P : (b + 1) * P], ident[:])
             return sums
 
-        def store(chunk, result):
-            nc.sync.dma_start(out[:, chunk * width : (chunk + 1) * width], result[:])
+        turned = psum.tile([P, OPENING], F32, name="turned", tag="narrow")
+        for r in reversed(range(TOP)):
+            add_turned(turned, gated_term(r, opening), r == TOP - 1, r == 0)
+        sums = turn_back(turned, "opening")
+        result = terms.tile([P, OPENING], F32, name="result_opening")
+        nc.scalar.copy(result[:], sums[:])
+        nc.sync.dma_start(out[:, :OPENING], result[:])
 
-        for chunk in range(chunks - DIRECT_CHUNKS):
-            sums = sum_terms(chunk, TOP)
-            result = pairs.tile([P, width], F32, name="result")
-            nc.scalar.copy(result[:], sums[:])
-            store(chunk, result)
-        closing = range(chunks - DIRECT_CHUNKS, chunks)
-        partial = [sum_terms(chunk, TOP - 1) for chunk in closing]
-        last_terms = [gated_term(TOP - 1, chunk) for chunk in closing]
-        for chunk, sums, term in zip(closing, partial, last_terms):
-            result = pairs.tile([P, width], F32, name="result")
+        chunks = [range(first, first + CHUNK) for first in range(OPENING, T, CHUNK)]
+        turned = [psum.tile([P, CHUNK], F32, name="turned", tag="narrow") for tokens in chunks]
+        for r in (3, 2):
+            term = gated_term(r, closing)
+            for bank, tokens in zip(turned, chunks):
+                add_turned(bank, term[:, tokens.start - OPENING : tokens.stop - OPENING], r == TOP - 1, False)
+        partial = []
+        for bank, tokens in zip(turned, chunks):
+            add_turned(bank, gated_term(1, tokens), False, True)
+            partial.append(turn_back(bank, "%d" % tokens.start))
+        last_terms = [gated_term(0, tokens) for tokens in chunks]
+        for tokens, sums, term in zip(chunks, partial, last_terms):
+            result = terms.tile([P, CHUNK], F32, name="result%d" % tokens.start)
             nc.vector.tensor_tensor(result[:], sums[:], term[:], ALU.add)
-            store(chunk, result)
+            nc.sync.dma_start(out[:, tokens.start : tokens.stop], result[:])

@@ -20,14 +20,15 @@ ACT = mybir.ActivationFunctionType
 
 P = 128
 PASSES = K // 512
-PIECE = 512
+PIECE = 256
+BY_PASS = (0, 10, 11)
+SHARED_FROM = 9
+EARLY_W2 = {5: (0, 1, 2, 3)}
+LATE_W2 = ((4,), (5, 6), (7, 8), (9,), (10,), (11,))
+LATE_ON_SCALAR = ((4,),)
+LATE_Y = ((4, 5, 6, 7), (8, 9, 10), (11,))
 OPENING = 512
 CHUNK = 256
-EARLY_W2 = {3: (0, 1, 2), 7: (3, 4, 5)}
-LATE_W2_LOADS = ((6,), (7, 8), (9,), (10,), (11,))
-LATE_Y = ((6, 7, 8), (9, 10), (11,))
-LAST_ON_VECTOR = 32
-SHARED_FROM = 9
 
 
 def tile_moe_ecr_mlp_relu2_kernel(
@@ -37,19 +38,15 @@ def tile_moe_ecr_mlp_relu2_kernel(
     with ExitStack() as ctx:
         lists = ctx.enter_context(tc.tile_pool(name="lists", bufs=1))
         keep = ctx.enter_context(tc.tile_pool(name="keep", bufs=1))
-        raws = ctx.enter_context(tc.tile_pool(name="raws", bufs=6))
-        work = ctx.enter_context(tc.tile_pool(name="work", bufs=4))
-        rounding = ctx.enter_context(tc.tile_pool(name="rounding", bufs=2))
-        late = ctx.enter_context(tc.tile_pool(name="late", bufs=1))
-        terms = ctx.enter_context(tc.tile_pool(name="terms", bufs=1))
+        raws = ctx.enter_context(tc.tile_pool(name="raws", bufs=7))
+        codes_ring = ctx.enter_context(tc.tile_pool(name="codes_ring", bufs=4))
+        twos = ctx.enter_context(tc.tile_pool(name="twos", bufs=2))
         psum = ctx.enter_context(tc.psum_pool(name="psum", bufs=4))
 
         token_scales = keep.tile([P, T], U8, name="token_scales", align_bytes=64)
         nc.vector.memset(token_scales[:].bitcast(I32), 0)
         y_all = keep.tile([P, SLOTS + PAD], F32, name="y_all")
         nc.vector.memset(y_all[:, SLOTS:], 0.0)
-        ident = keep.tile([P, P], F32, name="ident")
-        make_identity(nc, ident[:])
 
         token_words = []
         for o in range(PASSES):
@@ -60,25 +57,27 @@ def tile_moe_ecr_mlp_relu2_kernel(
                 offs_sb = lists.tile([P, SLOTS // 16], U16, name="offs_sb")
                 nc.sync.dma_start(offs_sb[:], offs)
         for q in range(4):
-            nc.scalar.dma_start(
-                token_scales[32 * q : 32 * q + 4 * PASSES, :].bitcast(I32),
-                x_scales[:, 4 * q : 4 * q + 4, :].bitcast(I32),
-            )
+            rows = slice(32 * q, 32 * q + 4 * PASSES)
+            scale_rows = raws.tile([P, T // 4], I32, name="raw", tag="raw", align_bytes=64)
+            nc.gpsimd.dma_start(scale_rows[rows, :], x_scales[:, 4 * q : 4 * q + 4, :].bitcast(I32))
+            nc.vector.tensor_copy(token_scales[rows, :].bitcast(I32), scale_rows[rows, :])
+        ident = keep.tile([P, P], F32, name="ident")
+        make_identity(nc, ident[:])
 
         slot_words, slot_scales = {}, {}
 
         def gather_tokens(piece):
             picks = offs_sb[:, piece * PIECE // 16 : (piece + 1) * PIECE // 16]
             for o in range(PASSES):
-                words = keep.tile([P, PIECE], U32, name="slot_words%d_%d" % (piece, o), align_bytes=64)
+                words = twos.tile([P, PIECE], U32, name="slot_words%d" % o, align_bytes=64)
                 nc.vector.tensor_copy(words[:], token_words[o][:].bitcast(U32).indirect(picks))
                 slot_words[piece, o] = words
-            scales = keep.tile([P, PIECE], U8, name="slot_scales%d" % piece, align_bytes=64)
+            scales = twos.tile([P, PIECE], U8, name="slot_scales", align_bytes=64)
             nc.vector.tensor_copy(scales[:], token_scales[:].indirect(picks))
             slot_scales[piece] = scales
 
         def load_w1(e, first, count):
-            raw = raws.tile([P, count, 4, H], F32, name="raw", tag="raw")
+            raw = raws.tile([P, count, 4, H], F32, name="raw", tag="raw", align_bytes=64)
             nc.sync.dma_start(
                 raw[:].rearrange("p o j i -> p o (j i)"),
                 w1[e, 512 * first : 512 * (first + count), :].rearrange("(o p j) i -> p o (j i)", p=P, j=4),
@@ -86,77 +85,84 @@ def tile_moe_ecr_mlp_relu2_kernel(
             return raw
 
         def quantize_w1(raw, count, on_vector):
-            source = raw[:].rearrange("p o j (m u v) -> p u o m j v", u=2, v=2)
-            halves = []
-            for u, split in enumerate((P, on_vector)):
-                rounded = rounding.tile([P, count, 2, P, 4], BF16, name="w1_rounded%d" % u, align_bytes=64)
-                target = rounded[:].rearrange("p o v m j -> p o m j v")
-                if split > 0:
-                    nc.vector.tensor_copy(target[:, :, :split], source[:, u, :, :split])
-                if split < P:
-                    nc.scalar.copy(target[:, :, split:], source[:, u, :, split:])
-                halves.append(rounded)
-            quantized = []
-            for u, rounded in enumerate(halves):
-                codes = work.tile([P, count, 2, P], U32, name="w1_codes%d" % u, align_bytes=64)
-                scales = work.tile([P, count, 2, P], U8, name="w1_scales%d" % u, align_bytes=64)
+            source = raw[:].rearrange("p o j (c v) -> p o c j v", v=4)
+            half = H // 2
+            rounded = [twos.tile([P, count, half, 4], BF16, name="w1_rounded%d" % u, align_bytes=64) for u in range(2)]
+            targets = [tile[:].rearrange("p o (c v) j -> p o c j v", v=4) for tile in rounded]
+            groups = half // 4
+            nc.vector.tensor_copy(targets[0], source[:, :, :groups])
+            if on_vector:
+                nc.vector.tensor_copy(targets[1][:, :, :on_vector], source[:, :, groups : groups + on_vector])
+            nc.scalar.copy(targets[1][:, :, on_vector:], source[:, :, groups + on_vector :])
+            made = []
+            for u, tile in enumerate(rounded):
+                codes = codes_ring.tile([P, count, half], U32, name="w1_codes%d" % u, align_bytes=64)
+                scales = codes_ring.tile([P, count, half], U8, name="w1_scales%d" % u, align_bytes=64)
                 nc.vector.quantize_mx(
-                    out=codes[:].rearrange("p o v m -> p (o v m)").bitcast(FP8X4),
-                    scales=scales[:].rearrange("p o v m -> p (o v m)"),
-                    in_=rounded[:].rearrange("p o v m j -> p (o v m j)"),
+                    out=codes[:].rearrange("p o i -> p (o i)").bitcast(FP8X4),
+                    scales=scales[:].rearrange("p o i -> p (o i)"),
+                    in_=tile[:].rearrange("p o i j -> p (o i j)"),
                 )
-                quantized.append((codes, scales))
-            return [[(codes[:, o], scales[:, o]) for codes, scales in quantized] for o in range(count)]
-
-        h_quantized = {}
+                made.append((codes, scales))
+            return [[(codes[:, o], scales[:, o]) for codes, scales in made] for o in range(count)]
 
         def first_product(e, w1_quantized):
             piece, first = divmod(e * C, PIECE)
             slots = slice(first, first + C)
-            a = psum.tile([P, 4, C], F32, name="a", tag="narrow")
+            a = psum.tile([P, 2, H // 2], F32, name="a", tag="first")
             for o in range(PASSES):
-                for t in range(4):
-                    u, v = divmod(t, 2)
+                for u in range(2):
                     codes, scales = w1_quantized[o][u]
                     nc.tensor.matmul_mx(
-                        out=a[:, t, :],
-                        lhsT=codes[:, v].bitcast(FP8X4),
-                        lhsT_scale=scales[:, v],
-                        rhs=slot_words[piece, o][:, slots].bitcast(FP8X4),
-                        rhs_scale=slot_scales[piece][4 * o :, slots],
-                        start=(o, t) == (0, 0),
-                        stop=(o, t) == (PASSES - 1, 3),
+                        out=a[:, u, :],
+                        lhsT=slot_words[piece, o][:, slots].bitcast(FP8X4),
+                        lhsT_scale=slot_scales[piece][4 * o :, slots],
+                        rhs=codes.bitcast(FP8X4),
+                        rhs_scale=scales,
+                        start=(o, u) == (0, 0),
+                        stop=(o, u) == (PASSES - 1, 1),
                     )
             return a
 
-        def quantize_h(e, a, positive):
-            nc.scalar.activation(positive.rearrange("p (c t) -> p c t", t=4), a[:].rearrange("p t c -> p c t"), ACT.Relu)
-            h = work.tile([P, C * 4], BF16, name="h", align_bytes=64)
-            nc.scalar.activation(h[:], positive, ACT.Square)
+        h_quantized = {}
+
+        def turn_h(a, positive):
+            nc.scalar.activation(
+                positive.rearrange("s (u g) (p v) -> s u g p v", u=2, v=2),
+                a[:].rearrange("s g (p u v) -> s u g p v", u=2, v=2),
+                ACT.Relu,
+            )
+            h_rows = twos.tile([P, 4, P], BF16, name="h_rows")
+            nc.scalar.activation(h_rows[:], positive, ACT.Square)
+            pairs = h_rows[:].rearrange("s r x -> s (r x)").bitcast(F32)
+            turned = psum.tile([P, 2, C], F32, name="h_turned", tag="second")
+            for u in range(2):
+                nc.tensor.transpose(turned[:, u, :], pairs[:, u * P : (u + 1) * P], ident[:])
+            return turned
+
+        def quantize_h(e, turned, h):
+            nc.scalar.copy(h.rearrange("p (s u) -> p s u", u=2), turned[:].rearrange("p u s -> p s u"))
             codes = keep.tile([P, C], U32, name="h_codes%d" % e, align_bytes=64)
             scales = keep.tile([P, C], U8, name="h_scales%d" % e, align_bytes=64)
-            nc.vector.quantize_mx(out=codes[:].bitcast(FP8X4), scales=scales[:], in_=h[:])
+            nc.vector.quantize_mx(out=codes[:].bitcast(FP8X4), scales=scales[:], in_=h.bitcast(BF16))
             h_quantized[e] = (codes, scales)
 
         w2_quantized = {}
 
-        def load_w2(experts):
-            raw = raws.tile([P, len(experts), 4, N], F32, name="raw", tag="raw")
+        def quantize_w2(experts, on_scalar):
+            count = len(experts)
+            raw = raws.tile([P, count, 4, N], F32, name="raw", tag="raw", align_bytes=64)
             nc.sync.dma_start(
                 raw[:].rearrange("p e j n -> p e (j n)"),
                 w2[experts[0] : experts[-1] + 1].rearrange("e (p j) n -> p e (j n)", j=4),
             )
-            return raw
-
-        def quantize_w2(experts, raw, pool, suffix, on_scalar=False):
-            count = len(experts)
-            rounded = pool.tile([P, count, N, 4], BF16, name="w2_rounded" + suffix, align_bytes=64)
+            rounded = keep.tile([P, count, N, 4], BF16, name="w2_rounded%d" % experts[0], align_bytes=64)
             target = rounded[:].rearrange("p e (c v) j -> p e c j v", v=4)
             source = raw[:].rearrange("p e j (c v) -> p e c j v", v=4)
             values = rounded[:].rearrange("p e n j -> p e (n j)")
-            codes = pool.tile([P, count, N], U32, name="w2_codes" + suffix, align_bytes=64)
-            scales = pool.tile([P, count, N], U8, name="w2_scales" + suffix, align_bytes=64)
-            for place, e in enumerate(experts):
+            codes = keep.tile([P, count, N], U32, name="w2_codes%d" % experts[0], align_bytes=64)
+            scales = keep.tile([P, count, N], U8, name="w2_scales%d" % experts[0], align_bytes=64)
+            for place in range(count):
                 if on_scalar:
                     nc.scalar.copy(target[:, place], source[:, place])
                 else:
@@ -166,7 +172,7 @@ def tile_moe_ecr_mlp_relu2_kernel(
                 w2_quantized[e] = (codes[:, place], scales[:, place])
 
         def second_layer(experts):
-            y = psum.tile([P, len(experts) * C], F32, name="y", tag="wide")
+            y = psum.tile([P, len(experts) * C], F32, name="y", tag="second")
             for place, e in enumerate(experts):
                 codes, scales = w2_quantized[e]
                 h_codes, h_scales = h_quantized[e]
@@ -182,21 +188,22 @@ def tile_moe_ecr_mlp_relu2_kernel(
             nc.scalar.copy(y_all[:, experts[0] * C : (experts[-1] + 1) * C], y[:])
 
         pos_sb = []
-        products = {}
+        products, turned = {}, {}
         for e in range(E):
             if e * C % PIECE == 0:
                 gather_tokens(e * C // PIECE)
-            share = LAST_ON_VECTOR if e >= SHARED_FROM else 0
-            if e in (0, E - 2, E - 1):
-                loaded = [load_w1(e, o, 1) for o in range(PASSES)]
-                w1_quantized = [
-                    quantize_w1(raw, 1, share)[0] for raw in loaded
-                ]
-            else:
-                loaded = [load_w1(e, 0, PASSES)]
-                w1_quantized = quantize_w1(loaded[0], PASSES, share)
+            share = 32 if e >= SHARED_FROM else 0
+            count = 1 if e in BY_PASS else PASSES
+            loaded = [load_w1(e, first, count) for first in range(0, PASSES, count)]
+            w1_quantized = [made for raw in loaded for made in quantize_w1(raw, count, share)]
+            if 1 < e <= SHARED_FROM:
+                quantize_h(e - 2, turned[e - 2], loaded[0][:, count - 1, 2, H // 2 :])
             if e > 0:
-                quantize_h(e - 1, products[e - 1], loaded[0][:, 0, 0, :])
+                turned[e - 1] = turn_h(products[e - 1], loaded[0][:, 0, :, H - P :])
+            if e > SHARED_FROM:
+                for done in range(len(h_quantized), e):
+                    words = twos.tile([P, H // 2], F32, name="h_words", align_bytes=64)
+                    quantize_h(done, turned[done], words[:])
             products[e] = first_product(e, w1_quantized)
             if e == 1:
                 for r, pos in enumerate((pos1, pos2, pos3, pos4)):
@@ -204,18 +211,18 @@ def tile_moe_ecr_mlp_relu2_kernel(
                     nc.sync.dma_start(tile[:], pos)
                     pos_sb.append(tile)
             if e in EARLY_W2:
-                quantize_w2(EARLY_W2[e], load_w2(EARLY_W2[e]), late, "_early")
+                quantize_w2(EARLY_W2[e], False)
                 second_layer(EARLY_W2[e])
-        last_positive = keep.tile([P, H], F32, name="last_positive")
-        quantize_h(E - 1, products[E - 1], last_positive[:])
-        for experts in LATE_W2_LOADS:
-            raw = load_w2(experts)
-            quantize_w2(experts, raw, late, "_%d" % experts[0], on_scalar=experts == LATE_W2_LOADS[0])
+        last_h = keep.tile([P, H // 2], F32, name="last_h", align_bytes=64)
+        last_positive = keep.tile([P, 4, P], F32, name="last_positive")
+        quantize_h(E - 1, turn_h(products[E - 1], last_positive[:]), last_h[:])
+        for experts in LATE_W2:
+            quantize_w2(experts, experts in LATE_ON_SCALAR)
         for experts in LATE_Y:
             second_layer(experts)
 
         def load_gate(ranks, tokens):
-            tile = raws.tile([P, len(ranks), len(tokens)], F32, name="raw", tag="raw")
+            tile = raws.tile([P, len(ranks), len(tokens)], F32, name="raw", tag="raw", align_bytes=64)
             nc.sync.dma_start(
                 tile[:], gate[ranks.start : ranks.stop, :, tokens.start : tokens.stop].rearrange("r n t -> n r t")
             )
@@ -230,7 +237,7 @@ def tile_moe_ecr_mlp_relu2_kernel(
         load_gate(range(0, 2), closing)
 
         def gated_term(r, tokens):
-            term = terms.tile([P, len(tokens)], F32, name="term%d_%d" % (r, tokens.start))
+            term = keep.tile([P, len(tokens)], F32, name="term%d_%d" % (r, tokens.start))
             picks = pos_sb[r][:, tokens.start // 16 : tokens.stop // 16]
             first = OPENING if tokens.start >= OPENING else 0
             factor = gates[r, tokens.start >= OPENING][:, tokens.start - first : tokens.stop - first]
@@ -251,23 +258,23 @@ def tile_moe_ecr_mlp_relu2_kernel(
 
         def turn_back(turned, name):
             width = turned.shape[1]
-            staged = terms.tile([P, width], F32, name="staged" + name)
+            staged = keep.tile([P, width], F32, name="staged" + name)
             nc.scalar.copy(staged[:], turned[:])
-            sums = psum.tile([P, width], F32, name="sums", tag="wide")
+            sums = psum.tile([P, width], F32, name="sums", tag="second")
             for b in range(width // P):
                 nc.tensor.transpose(sums[:, b * P : (b + 1) * P], staged[:, b * P : (b + 1) * P], ident[:])
             return sums
 
-        turned = psum.tile([P, OPENING], F32, name="turned", tag="narrow")
+        turned = psum.tile([P, OPENING], F32, name="turned", tag="first")
         for r in reversed(range(TOP)):
             add_turned(turned, gated_term(r, opening), r == TOP - 1, r == 0)
         sums = turn_back(turned, "opening")
-        result = terms.tile([P, OPENING], F32, name="result_opening")
+        result = keep.tile([P, OPENING], F32, name="result_opening")
         nc.scalar.copy(result[:], sums[:])
         nc.sync.dma_start(out[:, :OPENING], result[:])
 
         chunks = [range(first, first + CHUNK) for first in range(OPENING, T, CHUNK)]
-        turned = [psum.tile([P, CHUNK], F32, name="turned", tag="narrow") for tokens in chunks]
+        turned = [psum.tile([P, CHUNK], F32, name="turned", tag="first") for tokens in chunks]
         for r in (3, 2):
             term = gated_term(r, closing)
             for bank, tokens in zip(turned, chunks):
@@ -278,6 +285,6 @@ def tile_moe_ecr_mlp_relu2_kernel(
             partial.append(turn_back(bank, "%d" % tokens.start))
         last_terms = [gated_term(0, tokens) for tokens in chunks]
         for tokens, sums, term in zip(chunks, partial, last_terms):
-            result = terms.tile([P, CHUNK], F32, name="result%d" % tokens.start)
+            result = keep.tile([P, CHUNK], F32, name="result%d" % tokens.start)
             nc.vector.tensor_tensor(result[:], sums[:], term[:], ALU.add)
             nc.sync.dma_start(out[:, tokens.start : tokens.stop], result[:])

@@ -224,7 +224,7 @@ def tile_moe_ecr_mlp_relu2_kernel(
         def load_gate(ranks, tokens):
             tile = raws.tile([P, len(ranks), len(tokens)], F32, name="raw", tag="raw", align_bytes=64)
             nc.sync.dma_start(
-                tile[:], gate[ranks.start : ranks.stop, :, tokens.start : tokens.stop].rearrange("r n t -> n r t")
+                tile[:], gate[ranks.start : ranks.stop : ranks.step, :, tokens.start : tokens.stop].rearrange("r n t -> n r t")
             )
             for place, r in enumerate(ranks):
                 gates[r, tokens.start >= OPENING] = tile[:, place, :]
@@ -233,15 +233,28 @@ def tile_moe_ecr_mlp_relu2_kernel(
         gates = {}
         load_gate(range(3, 4), opening)
         load_gate(range(0, 3), opening)
-        load_gate(range(2, 4), closing)
-        load_gate(range(0, 2), closing)
+        load_gate(range(0, 4, 3), closing)
+        load_gate(range(1, 3), closing)
+
+        def picked(r, tokens):
+            return y_all[:].indirect(pos_sb[r][:, tokens.start // 16 : tokens.stop // 16])
+
+        fetched = {}
+        for tokens in (opening, closing):
+            term = keep.tile([P, len(tokens)], F32, name="fetched%d" % tokens.start)
+            nc.scalar.activation(term[:], picked(0, tokens), ACT.Copy)
+            fetched[tokens.start] = term
+
+        def weighed(tokens):
+            term = fetched[tokens.start]
+            nc.vector.tensor_tensor(term[:], term[:], gates[0, tokens.start >= OPENING], ALU.mult)
+            return term
 
         def gated_term(r, tokens):
             term = keep.tile([P, len(tokens)], F32, name="term%d_%d" % (r, tokens.start))
-            picks = pos_sb[r][:, tokens.start // 16 : tokens.stop // 16]
             first = OPENING if tokens.start >= OPENING else 0
             factor = gates[r, tokens.start >= OPENING][:, tokens.start - first : tokens.stop - first]
-            nc.vector.tensor_tensor(term[:], y_all[:].indirect(picks), factor, ALU.mult)
+            nc.vector.tensor_tensor(term[:], picked(r, tokens), factor, ALU.mult)
             return term
 
         def add_turned(turned, term, start, stop):
@@ -267,7 +280,7 @@ def tile_moe_ecr_mlp_relu2_kernel(
 
         turned = psum.tile([P, OPENING], F32, name="turned", tag="first")
         for r in reversed(range(TOP)):
-            add_turned(turned, gated_term(r, opening), r == TOP - 1, r == 0)
+            add_turned(turned, gated_term(r, opening) if r else weighed(opening), r == TOP - 1, r == 0)
         sums = turn_back(turned, "opening")
         result = keep.tile([P, OPENING], F32, name="result_opening")
         nc.scalar.copy(result[:], sums[:])
@@ -275,15 +288,15 @@ def tile_moe_ecr_mlp_relu2_kernel(
 
         chunks = [range(first, first + CHUNK) for first in range(OPENING, T, CHUNK)]
         turned = [psum.tile([P, CHUNK], F32, name="turned", tag="first") for tokens in chunks]
-        for r in (3, 2):
-            term = gated_term(r, closing)
+        for r in (3, 0):
+            term = gated_term(r, closing) if r else weighed(closing)
             for bank, tokens in zip(turned, chunks):
                 add_turned(bank, term[:, tokens.start - OPENING : tokens.stop - OPENING], r == TOP - 1, False)
         partial = []
         for bank, tokens in zip(turned, chunks):
-            add_turned(bank, gated_term(1, tokens), False, True)
+            add_turned(bank, gated_term(2, tokens), False, True)
             partial.append(turn_back(bank, "%d" % tokens.start))
-        last_terms = [gated_term(0, tokens) for tokens in chunks]
+        last_terms = [gated_term(1, tokens) for tokens in chunks]
         for tokens, sums, term in zip(chunks, partial, last_terms):
             result = keep.tile([P, CHUNK], F32, name="result%d" % tokens.start)
             nc.vector.tensor_tensor(result[:], sums[:], term[:], ALU.add)

@@ -24,8 +24,9 @@ PIECE = 256
 BY_PASS = (0, 10, 11)
 SHARED_FROM = 9
 EARLY_W2 = {5: (0, 1, 2, 3)}
-LATE_W2 = ((4,), (5, 6), (7, 8), (9,), (10,), (11,))
-LATE_ON_SCALAR = ((4,),)
+LATE_W2 = ((4,), (5, 6), (7,), (8,), (9, 10), (11,))
+LATE_ON_SCALAR = ((4,), (8,))
+VECTOR_ALONE = (10, 0)
 LATE_Y = ((4, 5, 6, 7), (8, 9, 10), (11,))
 OPENING = 512
 CHUNK = 256
@@ -84,16 +85,17 @@ def tile_moe_ecr_mlp_relu2_kernel(
             )
             return raw
 
-        def quantize_w1(raw, count, on_vector):
+        def quantize_w1(raw, count, vector_alone):
             source = raw[:].rearrange("p o j (c v) -> p o c j v", v=4)
             half = H // 2
             rounded = [twos.tile([P, count, half, 4], BF16, name="w1_rounded%d" % u, align_bytes=64) for u in range(2)]
             targets = [tile[:].rearrange("p o (c v) j -> p o c j v", v=4) for tile in rounded]
             groups = half // 4
             nc.vector.tensor_copy(targets[0], source[:, :, :groups])
-            if on_vector:
-                nc.vector.tensor_copy(targets[1][:, :, :on_vector], source[:, :, groups : groups + on_vector])
-            nc.scalar.copy(targets[1][:, :, on_vector:], source[:, :, groups + on_vector :])
+            if vector_alone:
+                nc.vector.tensor_copy(targets[1], source[:, :, groups:])
+            else:
+                nc.scalar.copy(targets[1], source[:, :, groups:])
             made = []
             for u, tile in enumerate(rounded):
                 codes = codes_ring.tile([P, count, half], U32, name="w1_codes%d" % u, align_bytes=64)
@@ -127,48 +129,52 @@ def tile_moe_ecr_mlp_relu2_kernel(
         h_quantized = {}
 
         def turn_h(a, positive):
-            nc.scalar.activation(
-                positive.rearrange("s (u g) (p v) -> s u g p v", u=2, v=2),
-                a[:].rearrange("s g (p u v) -> s u g p v", u=2, v=2),
-                ACT.Relu,
-            )
-            h_rows = twos.tile([P, 4, P], BF16, name="h_rows")
-            nc.scalar.activation(h_rows[:], positive, ACT.Square)
-            pairs = h_rows[:].rearrange("s r x -> s (r x)").bitcast(F32)
-            turned = psum.tile([P, 2, C], F32, name="h_turned", tag="second")
-            for u in range(2):
-                nc.tensor.transpose(turned[:, u, :], pairs[:, u * P : (u + 1) * P], ident[:])
+            nc.scalar.activation(positive, a[:].rearrange("s g (p j) -> s j (g p)", j=4), ACT.Relu)
+            turned = psum.tile([P, 4, C], F32, name="h_turned", tag="second")
+            for j in range(4):
+                nc.tensor.transpose(turned[:, j, :], positive[:, j, :], ident[:])
             return turned
 
-        def quantize_h(e, turned, h):
-            nc.scalar.copy(h.rearrange("p (s u) -> p s u", u=2), turned[:].rearrange("p u s -> p s u"))
-            codes = keep.tile([P, C], U32, name="h_codes%d" % e, align_bytes=64)
+        def square_h(turned, h):
+            values = h.bitcast(BF16)
+            nc.scalar.activation(values.rearrange("p (s j) -> p s j", j=4), turned[:].rearrange("p j s -> p s j"), ACT.Square)
+            return values
+
+        def quantize_h(e, values):
+            room = "w2_rounded%d" % e if e == E - 1 else "h_codes%d" % e
+            codes = keep.tile([P, C], U32, name="h_codes", tag=room, align_bytes=64)
             scales = keep.tile([P, C], U8, name="h_scales%d" % e, align_bytes=64)
-            nc.vector.quantize_mx(out=codes[:].bitcast(FP8X4), scales=scales[:], in_=h.bitcast(BF16))
+            nc.vector.quantize_mx(out=codes[:].bitcast(FP8X4), scales=scales[:], in_=values)
             h_quantized[e] = (codes, scales)
 
         w2_quantized = {}
 
-        def quantize_w2(experts, on_scalar):
+        def round_w2(experts, on_scalar):
             count = len(experts)
             raw = raws.tile([P, count, 4, N], F32, name="raw", tag="raw", align_bytes=64)
             nc.sync.dma_start(
                 raw[:].rearrange("p e j n -> p e (j n)"),
                 w2[experts[0] : experts[-1] + 1].rearrange("e (p j) n -> p e (j n)", j=4),
             )
-            rounded = keep.tile([P, count, N, 4], BF16, name="w2_rounded%d" % experts[0], align_bytes=64)
+            rounded = keep.tile([P, count, N, 4], BF16, name="w2_rounded", tag="w2_rounded%d" % experts[0], align_bytes=64)
             target = rounded[:].rearrange("p e (c v) j -> p e c j v", v=4)
             source = raw[:].rearrange("p e j (c v) -> p e c j v", v=4)
-            values = rounded[:].rearrange("p e n j -> p e (n j)")
+            if on_scalar:
+                nc.scalar.copy(target, source)
+            else:
+                nc.vector.tensor_copy(target, source)
+            return rounded
+
+        def quantize_w2(experts, rounded):
+            count = len(experts)
             codes = keep.tile([P, count, N], U32, name="w2_codes%d" % experts[0], align_bytes=64)
             scales = keep.tile([P, count, N], U8, name="w2_scales%d" % experts[0], align_bytes=64)
-            for place in range(count):
-                if on_scalar:
-                    nc.scalar.copy(target[:, place], source[:, place])
-                else:
-                    nc.vector.tensor_copy(target[:, place], source[:, place])
+            nc.vector.quantize_mx(
+                out=codes[:].rearrange("p e n -> p (e n)").bitcast(FP8X4),
+                scales=scales[:].rearrange("p e n -> p (e n)"),
+                in_=rounded[:].rearrange("p e n j -> p (e n j)"),
+            )
             for place, e in enumerate(experts):
-                nc.vector.quantize_mx(out=codes[:, place].bitcast(FP8X4), scales=scales[:, place], in_=values[:, place])
                 w2_quantized[e] = (codes[:, place], scales[:, place])
 
         def second_layer(experts):
@@ -192,18 +198,19 @@ def tile_moe_ecr_mlp_relu2_kernel(
         for e in range(E):
             if e * C % PIECE == 0:
                 gather_tokens(e * C // PIECE)
-            share = 32 if e >= SHARED_FROM else 0
             count = 1 if e in BY_PASS else PASSES
             loaded = [load_w1(e, first, count) for first in range(0, PASSES, count)]
-            w1_quantized = [made for raw in loaded for made in quantize_w1(raw, count, share)]
+            w1_quantized = [
+                made for o, raw in enumerate(loaded) for made in quantize_w1(raw, count, (e, o) == VECTOR_ALONE)
+            ]
             if 1 < e <= SHARED_FROM:
-                quantize_h(e - 2, turned[e - 2], loaded[0][:, count - 1, 2, H // 2 :])
+                quantize_h(e - 2, square_h(turned[e - 2], loaded[0][:, count - 1, 2, H // 2 :]))
             if e > 0:
                 turned[e - 1] = turn_h(products[e - 1], loaded[0][:, 0, :, H - P :])
             if e > SHARED_FROM:
                 for done in range(len(h_quantized), e):
                     words = twos.tile([P, H // 2], F32, name="h_words", align_bytes=64)
-                    quantize_h(done, turned[done], words[:])
+                    quantize_h(done, square_h(turned[done], words[:]))
             products[e] = first_product(e, w1_quantized)
             if e == 1:
                 for r, pos in enumerate((pos1, pos2, pos3, pos4)):
@@ -211,13 +218,18 @@ def tile_moe_ecr_mlp_relu2_kernel(
                     nc.sync.dma_start(tile[:], pos)
                     pos_sb.append(tile)
             if e in EARLY_W2:
-                quantize_w2(EARLY_W2[e], False)
+                quantize_w2(EARLY_W2[e], round_w2(EARLY_W2[e], False))
                 second_layer(EARLY_W2[e])
         last_h = keep.tile([P, H // 2], F32, name="last_h", align_bytes=64)
         last_positive = keep.tile([P, 4, P], F32, name="last_positive")
-        quantize_h(E - 1, turn_h(products[E - 1], last_positive[:]), last_h[:])
+        last_values = square_h(turn_h(products[E - 1], last_positive[:]), last_h[:])
+        waiting = []
         for experts in LATE_W2:
-            quantize_w2(experts, experts in LATE_ON_SCALAR)
+            waiting.append((experts, round_w2(experts, experts in LATE_ON_SCALAR)))
+            if len(waiting) == 2:
+                quantize_w2(*waiting.pop(0))
+        quantize_w2(*waiting.pop(0))
+        quantize_h(E - 1, last_values)
         for experts in LATE_Y:
             second_layer(experts)
 

@@ -28,8 +28,7 @@ LATE_W2 = ((4,), (5, 6), (7,), (8,), (9, 10), (11,))
 LATE_ON_SCALAR = ((4,), (8,))
 VECTOR_ALONE = (10, 0)
 LATE_Y = ((4, 5, 6, 7), (8, 9, 10), (11,))
-OPENING = 512
-CHUNK = 256
+FIRST, SECOND, THIRD, FOURTH = range(0, 256), range(256, 768), range(768, 1024), range(1024, 1280)
 
 
 def tile_moe_ecr_mlp_relu2_kernel(
@@ -239,34 +238,37 @@ def tile_moe_ecr_mlp_relu2_kernel(
                 tile[:], gate[ranks.start : ranks.stop : ranks.step, :, tokens.start : tokens.stop].rearrange("r n t -> n r t")
             )
             for place, r in enumerate(ranks):
-                gates[r, tokens.start >= OPENING] = tile[:, place, :]
+                gates[r, tokens.start] = tile[:, place, :]
 
-        opening, closing = range(0, OPENING), range(OPENING, T)
         gates = {}
-        load_gate(range(3, 4), opening)
-        load_gate(range(0, 3), opening)
-        load_gate(range(0, 4, 3), closing)
-        load_gate(range(1, 3), closing)
+        early, late = range(FIRST.start, SECOND.stop), range(THIRD.start, FOURTH.stop)
+        load_gate(range(2, 4), FIRST)
+        load_gate(range(2, 4), SECOND)
+        load_gate(range(0, 2), early)
+        load_gate(range(0, 4, 3), late)
+        load_gate(range(1, 3), late)
+
+        def gate_of(r, tokens):
+            first = max(start for rank, start in gates if rank == r and start <= tokens.start)
+            return gates[r, first][:, tokens.start - first : tokens.stop - first]
 
         def picked(r, tokens):
             return y_all[:].indirect(pos_sb[r][:, tokens.start // 16 : tokens.stop // 16])
 
         fetched = {}
-        for tokens in (opening, closing):
+        for tokens in (FIRST, SECOND, late):
             term = keep.tile([P, len(tokens)], F32, name="fetched%d" % tokens.start)
             nc.scalar.activation(term[:], picked(0, tokens), ACT.Copy)
             fetched[tokens.start] = term
 
         def weighed(tokens):
             term = fetched[tokens.start]
-            nc.vector.tensor_tensor(term[:], term[:], gates[0, tokens.start >= OPENING], ALU.mult)
+            nc.vector.tensor_tensor(term[:], term[:], gate_of(0, tokens), ALU.mult)
             return term
 
         def gated_term(r, tokens):
             term = keep.tile([P, len(tokens)], F32, name="term%d_%d" % (r, tokens.start))
-            first = OPENING if tokens.start >= OPENING else 0
-            factor = gates[r, tokens.start >= OPENING][:, tokens.start - first : tokens.stop - first]
-            nc.vector.tensor_tensor(term[:], picked(r, tokens), factor, ALU.mult)
+            nc.vector.tensor_tensor(term[:], picked(r, tokens), gate_of(r, tokens), ALU.mult)
             return term
 
         def add_turned(turned, term, start, stop):
@@ -290,26 +292,33 @@ def tile_moe_ecr_mlp_relu2_kernel(
                 nc.tensor.transpose(sums[:, b * P : (b + 1) * P], staged[:, b * P : (b + 1) * P], ident[:])
             return sums
 
-        turned = psum.tile([P, OPENING], F32, name="turned", tag="first")
-        for r in reversed(range(TOP)):
-            add_turned(turned, gated_term(r, opening) if r else weighed(opening), r == TOP - 1, r == 0)
-        sums = turn_back(turned, "opening")
-        result = keep.tile([P, OPENING], F32, name="result_opening")
-        nc.scalar.copy(result[:], sums[:])
-        nc.sync.dma_start(out[:, :OPENING], result[:])
-
-        chunks = [range(first, first + CHUNK) for first in range(OPENING, T, CHUNK)]
-        turned = [psum.tile([P, CHUNK], F32, name="turned", tag="first") for tokens in chunks]
-        for r in (3, 0):
-            term = gated_term(r, closing) if r else weighed(closing)
-            for bank, tokens in zip(turned, chunks):
-                add_turned(bank, term[:, tokens.start - OPENING : tokens.stop - OPENING], r == TOP - 1, False)
-        partial = []
-        for bank, tokens in zip(turned, chunks):
-            add_turned(bank, gated_term(2, tokens), False, True)
-            partial.append(turn_back(bank, "%d" % tokens.start))
-        last_terms = [gated_term(1, tokens) for tokens in chunks]
-        for tokens, sums, term in zip(chunks, partial, last_terms):
-            result = keep.tile([P, CHUNK], F32, name="result%d" % tokens.start)
+        def close(tokens, sums, term):
+            result = keep.tile([P, len(tokens)], F32, name="result%d" % tokens.start)
             nc.vector.tensor_tensor(result[:], sums[:], term[:], ALU.add)
             nc.sync.dma_start(out[:, tokens.start : tokens.stop], result[:])
+
+        turned = {
+            tokens.start: psum.tile([P, len(tokens)], F32, name="turned", tag="first")
+            for tokens in (FIRST, SECOND, THIRD, FOURTH)
+        }
+        sums, last_terms = {}, {}
+        for tokens in (FIRST, SECOND):
+            for r in (3, 2):
+                add_turned(turned[tokens.start], gated_term(r, tokens), r == 3, False)
+        for tokens in (FIRST, SECOND):
+            add_turned(turned[tokens.start], weighed(tokens), False, True)
+            sums[tokens.start] = turn_back(turned[tokens.start], "%d" % tokens.start)
+        last_terms[FIRST.start] = gated_term(1, FIRST)
+        for term, start in ((gated_term(3, late), True), (weighed(late), False)):
+            for tokens in (THIRD, FOURTH):
+                add_turned(turned[tokens.start], term[:, tokens.start - late.start : tokens.stop - late.start], start, False)
+        close(FIRST, sums[FIRST.start], last_terms[FIRST.start])
+        for tokens in (THIRD, FOURTH):
+            add_turned(turned[tokens.start], gated_term(2, tokens), False, True)
+            sums[tokens.start] = turn_back(turned[tokens.start], "%d" % tokens.start)
+        last_terms[SECOND.start] = gated_term(1, SECOND)
+        last_terms[THIRD.start] = gated_term(1, THIRD)
+        close(SECOND, sums[SECOND.start], last_terms[SECOND.start])
+        last_terms[FOURTH.start] = gated_term(1, FOURTH)
+        for tokens in (THIRD, FOURTH):
+            close(tokens, sums[tokens.start], last_terms[tokens.start])

@@ -64,6 +64,27 @@ def tile_moe_ecr_mlp_relu2_kernel(
         ident = keep.tile([P, P], F32, name="ident")
         make_identity(nc, ident[:])
 
+        blocks = T // P
+        gate_rows = keep.tile([P, P], F32, name="gate_rows")
+        nc.vector.memset(gate_rows[:], 0.0)
+        for r in range(TOP):
+            nc.scalar.dma_start(gate_rows[r * blocks : (r + 1) * blocks, :], gate[r, 0].rearrange("(b t) -> b t", t=P))
+        gate_turned = psum.tile([P, P], F32, name="gate_turned", tag="second")
+        nc.tensor.transpose(gate_turned[:], gate_rows[:], ident[:])
+        gate_columns = keep.tile([P, TOP * blocks], F32, name="gate_columns")
+        nc.scalar.copy(gate_columns[:], gate_turned[:, : TOP * blocks])
+        gates = keep.tile([P, TOP * T], F32, name="gates")
+
+        def spread_gate(first):
+            bank = psum.tile([P, 4, P], F32, name="gate_spread", tag="first")
+            for b in range(4):
+                column = gate_columns[:, first + b : first + b + 1]
+                nc.tensor.transpose(bank[:, b, :], column.to_broadcast([P, P]), ident[:])
+            nc.scalar.copy(gates[:, first * P : (first + 4) * P], bank[:].rearrange("p b t -> p (b t)"))
+
+        for first in range(0, TOP * blocks, 4):
+            spread_gate(first)
+
         slot_words, slot_scales = {}, {}
 
         def gather_tokens(piece):
@@ -232,43 +253,26 @@ def tile_moe_ecr_mlp_relu2_kernel(
         for experts in LATE_Y:
             second_layer(experts)
 
-        def load_gate(ranks, tokens):
-            tile = raws.tile([P, len(ranks), len(tokens)], F32, name="raw", tag="raw", align_bytes=64)
-            nc.sync.dma_start(
-                tile[:], gate[ranks.start : ranks.stop : ranks.step, :, tokens.start : tokens.stop].rearrange("r n t -> n r t")
-            )
-            for place, r in enumerate(ranks):
-                gates[r, tokens.start] = tile[:, place, :]
-
-        gates = {}
-        early, late = range(FIRST.start, SECOND.stop), range(THIRD.start, FOURTH.stop)
-        load_gate(range(2, 4), FIRST)
-        load_gate(range(2, 4), SECOND)
-        load_gate(range(0, 2), early)
-        load_gate(range(0, 4, 3), late)
-        load_gate(range(1, 3), late)
+        late = range(THIRD.start, FOURTH.stop)
 
         def gate_of(r, tokens):
-            first = max(start for rank, start in gates if rank == r and start <= tokens.start)
-            return gates[r, first][:, tokens.start - first : tokens.stop - first]
+            return gates[:, r * T + tokens.start : r * T + tokens.stop]
 
         def picked(r, tokens):
             return y_all[:].indirect(pos_sb[r][:, tokens.start // 16 : tokens.stop // 16])
 
-        fetched = {}
+        terms = [raws.tile([P, T], F32, name="raw", tag="raw", align_bytes=64) for r in range(TOP)]
         for tokens in (FIRST, SECOND, late):
-            term = keep.tile([P, len(tokens)], F32, name="fetched%d" % tokens.start)
-            nc.scalar.activation(term[:], picked(0, tokens), ACT.Copy)
-            fetched[tokens.start] = term
+            nc.scalar.activation(terms[0][:, tokens.start : tokens.stop], picked(0, tokens), ACT.Copy)
 
         def weighed(tokens):
-            term = fetched[tokens.start]
-            nc.vector.tensor_tensor(term[:], term[:], gate_of(0, tokens), ALU.mult)
+            term = terms[0][:, tokens.start : tokens.stop]
+            nc.vector.tensor_tensor(term, term, gate_of(0, tokens), ALU.mult)
             return term
 
         def gated_term(r, tokens):
-            term = keep.tile([P, len(tokens)], F32, name="term%d_%d" % (r, tokens.start))
-            nc.vector.tensor_tensor(term[:], picked(r, tokens), gate_of(r, tokens), ALU.mult)
+            term = terms[r][:, tokens.start : tokens.stop]
+            nc.vector.tensor_tensor(term, picked(r, tokens), gate_of(r, tokens), ALU.mult)
             return term
 
         def add_turned(turned, term, start, stop):
@@ -294,7 +298,7 @@ def tile_moe_ecr_mlp_relu2_kernel(
 
         def close(tokens, sums, term):
             result = keep.tile([P, len(tokens)], F32, name="result%d" % tokens.start)
-            nc.vector.tensor_tensor(result[:], sums[:], term[:], ALU.add)
+            nc.vector.tensor_tensor(result[:], sums[:], term, ALU.add)
             nc.sync.dma_start(out[:, tokens.start : tokens.stop], result[:])
 
         turned = {

@@ -28,7 +28,8 @@ LATE_W2 = ((4,), (5, 6), (7,), (8,), (9, 10), (11,))
 LATE_ON_SCALAR = ((4,), (8,))
 VECTOR_ALONE = (10, 0)
 LATE_Y = ((4, 5, 6, 7), (8, 9, 10), (11,))
-FIRST, SECOND, THIRD, FOURTH = range(0, 256), range(256, 768), range(768, 1024), range(1024, 1280)
+ONE_PLAIN = (range(0, 256), range(256, 640))
+TWO_PLAIN = (range(640, 1024), range(1024, 1280))
 
 
 def tile_moe_ecr_mlp_relu2_kernel(
@@ -41,7 +42,16 @@ def tile_moe_ecr_mlp_relu2_kernel(
         raws = ctx.enter_context(tc.tile_pool(name="raws", bufs=7))
         codes_ring = ctx.enter_context(tc.tile_pool(name="codes_ring", bufs=4))
         twos = ctx.enter_context(tc.tile_pool(name="twos", bufs=2))
-        psum = ctx.enter_context(tc.psum_pool(name="psum", bufs=4))
+        psum = ctx.enter_context(tc.psum_pool(name="psum", bufs=1))
+        turns = {"first": [], "second": []}
+
+        def bank(number, shape, name):
+            return psum.tile(shape, F32, name=name, tag="bank%d" % number)
+
+        def next_bank(ring, shape, name):
+            turns[ring].append(name)
+            return bank((len(turns[ring]) - 1) % 4 + (4 if ring == "second" else 0), shape, name)
+
 
         token_scales = keep.tile([P, T], U8, name="token_scales", align_bytes=64)
         nc.vector.memset(token_scales[:].bitcast(I32), 0)
@@ -69,21 +79,19 @@ def tile_moe_ecr_mlp_relu2_kernel(
         nc.vector.memset(gate_rows[:], 0.0)
         for r in range(TOP):
             nc.scalar.dma_start(gate_rows[r * blocks : (r + 1) * blocks, :], gate[r, 0].rearrange("(b t) -> b t", t=P))
-        gate_turned = psum.tile([P, P], F32, name="gate_turned", tag="second")
+        gate_turned = next_bank("second", [P, P], "gate_turned")
         nc.tensor.transpose(gate_turned[:], gate_rows[:], ident[:])
         gate_columns = keep.tile([P, TOP * blocks], F32, name="gate_columns")
         nc.scalar.copy(gate_columns[:], gate_turned[:, : TOP * blocks])
-        gates = keep.tile([P, TOP * T], F32, name="gates")
-
-        def spread_gate(first):
-            bank = psum.tile([P, 4, P], F32, name="gate_spread", tag="first")
-            for b in range(4):
-                column = gate_columns[:, first + b : first + b + 1]
-                nc.tensor.transpose(bank[:, b, :], column.to_broadcast([P, P]), ident[:])
-            nc.scalar.copy(gates[:, first * P : (first + 4) * P], bank[:].rearrange("p b t -> p (b t)"))
-
-        for first in range(0, TOP * blocks, 4):
-            spread_gate(first)
+        spread_blocks = [(r, b) for r in range(TOP) for b in range(blocks) if r > 1 or b < TWO_PLAIN[0].start // P]
+        gates = keep.tile([P, len(spread_blocks) * P], F32, name="gates")
+        for first in range(0, len(spread_blocks), 4):
+            group = spread_blocks[first : first + 4]
+            spread = next_bank("first", [P, len(group), P], "gate_spread")
+            for place, (r, b) in enumerate(group):
+                column = gate_columns[:, r * blocks + b : r * blocks + b + 1]
+                nc.tensor.transpose(spread[:, place, :], column.to_broadcast([P, P]), ident[:])
+            nc.scalar.copy(gates[:, first * P : (first + len(group)) * P], spread[:].rearrange("p b t -> p (b t)"))
 
         slot_words, slot_scales = {}, {}
 
@@ -131,7 +139,7 @@ def tile_moe_ecr_mlp_relu2_kernel(
         def first_product(e, w1_quantized):
             piece, first = divmod(e * C, PIECE)
             slots = slice(first, first + C)
-            a = psum.tile([P, 2, H // 2], F32, name="a", tag="first")
+            a = next_bank("first", [P, 2, H // 2], "a")
             for o in range(PASSES):
                 for u in range(2):
                     codes, scales = w1_quantized[o][u]
@@ -150,7 +158,7 @@ def tile_moe_ecr_mlp_relu2_kernel(
 
         def turn_h(a, positive):
             nc.scalar.activation(positive, a[:].rearrange("s g (p j) -> s j (g p)", j=4), ACT.Relu)
-            turned = psum.tile([P, 4, C], F32, name="h_turned", tag="second")
+            turned = next_bank("second", [P, 4, C], "h_turned")
             for j in range(4):
                 nc.tensor.transpose(turned[:, j, :], positive[:, j, :], ident[:])
             return turned
@@ -198,7 +206,7 @@ def tile_moe_ecr_mlp_relu2_kernel(
                 w2_quantized[e] = (codes[:, place], scales[:, place])
 
         def second_layer(experts):
-            y = psum.tile([P, len(experts) * C], F32, name="y", tag="second")
+            y = next_bank("second", [P, len(experts) * C], "y")
             for place, e in enumerate(experts):
                 codes, scales = w2_quantized[e]
                 h_codes, h_scales = h_quantized[e]
@@ -253,76 +261,102 @@ def tile_moe_ecr_mlp_relu2_kernel(
         for experts in LATE_Y:
             second_layer(experts)
 
-        late = range(THIRD.start, FOURTH.stop)
-
-        def gate_of(r, tokens):
-            return gates[:, r * T + tokens.start : r * T + tokens.stop]
+        terms = [raws.tile([P, T], F32, name="raw", tag="raw", align_bytes=64) for r in range(TOP)]
+        staged = [raws.tile([P, T], F32, name="raw", tag="raw", align_bytes=64) for r in range(2)]
+        result = keep.tile([P, T], F32, name="result")
 
         def picked(r, tokens):
             return y_all[:].indirect(pos_sb[r][:, tokens.start // 16 : tokens.stop // 16])
 
-        terms = [raws.tile([P, T], F32, name="raw", tag="raw", align_bytes=64) for r in range(TOP)]
-        for tokens in (FIRST, SECOND, late):
-            nc.scalar.activation(terms[0][:, tokens.start : tokens.stop], picked(0, tokens), ACT.Copy)
+        def columns(tile, tokens):
+            return tile[:, tokens.start : tokens.stop]
 
-        def weighed(tokens):
-            term = terms[0][:, tokens.start : tokens.stop]
-            nc.vector.tensor_tensor(term, term, gate_of(0, tokens), ALU.mult)
-            return term
+        def block(tile, b):
+            return tile[:, b * P : (b + 1) * P]
 
-        def gated_term(r, tokens):
-            term = terms[r][:, tokens.start : tokens.stop]
-            nc.vector.tensor_tensor(term, picked(r, tokens), gate_of(r, tokens), ALU.mult)
-            return term
+        def blocks_of(tokens):
+            return range(tokens.start // P, tokens.stop // P)
 
-        def add_turned(turned, term, start, stop):
-            blocks = turned.shape[1] // P
-            for b in range(blocks):
+        def gate_of(r, tokens):
+            first = spread_blocks.index((r, tokens.start // P)) * P
+            return gates[:, first : first + len(tokens)]
+
+        def turn(into, sources, tokens, start, stop):
+            steps = [(source, b) for source in sources for b in blocks_of(tokens)]
+            for step, (source, b) in enumerate(steps):
                 nc.tensor.matmul(
-                    turned[:, b * P : (b + 1) * P],
-                    lhsT=term[:, b * P : (b + 1) * P],
+                    block(into, b - tokens.start // P),
+                    lhsT=block(source, b),
                     rhs=ident[:],
                     is_transpose=True,
-                    start=start and b == 0,
-                    stop=stop and b == blocks - 1,
+                    start=start and step == 0,
+                    stop=stop and step == len(steps) - 1,
                 )
 
-        def turn_back(turned, name):
-            width = turned.shape[1]
-            staged = keep.tile([P, width], F32, name="staged" + name)
-            nc.scalar.copy(staged[:], turned[:])
-            sums = psum.tile([P, width], F32, name="sums", tag="second")
-            for b in range(width // P):
-                nc.tensor.transpose(sums[:, b * P : (b + 1) * P], staged[:, b * P : (b + 1) * P], ident[:])
+        def plain_term(r, tokens):
+            nc.scalar.activation(columns(terms[r], tokens), picked(r, tokens), ACT.Copy)
+
+        def gated_term(r, tokens, into):
+            nc.vector.tensor_tensor(into, picked(r, tokens), gate_of(r, tokens), ALU.mult)
+            return into
+
+        def three_turned(number, tokens):
+            turned = bank(number, [P, len(tokens)], "turned")
+            for r in (3, 2):
+                gated_term(r, tokens, columns(terms[r], tokens))
+                turn(turned, [terms[r]], tokens, r == 3, False)
+            nc.vector.tensor_tensor(columns(terms[0], tokens), columns(terms[0], tokens), gate_of(0, tokens), ALU.mult)
+            turn(turned, [terms[0]], tokens, False, True)
+            return turned
+
+        def turn_back(number, turned, tokens):
+            nc.scalar.copy(columns(staged[0], tokens), turned[:])
+            sums = bank(number, [P, len(tokens)], "sums")
+            turn(sums, staged[:1], tokens, True, True)
             return sums
 
-        def close(tokens, sums, term):
-            result = keep.tile([P, len(tokens)], F32, name="result%d" % tokens.start)
-            nc.vector.tensor_tensor(result[:], sums[:], term, ALU.add)
-            nc.sync.dma_start(out[:, tokens.start : tokens.stop], result[:])
+        def two_turned(into, tokens):
+            for r in range(2):
+                plain_term(r, tokens)
+                turn(into[r], [terms[r]], tokens, True, True)
 
-        turned = {
-            tokens.start: psum.tile([P, len(tokens)], F32, name="turned", tag="first")
-            for tokens in (FIRST, SECOND, THIRD, FOURTH)
-        }
-        sums, last_terms = {}, {}
-        for tokens in (FIRST, SECOND):
-            for r in (3, 2):
-                add_turned(turned[tokens.start], gated_term(r, tokens), r == 3, False)
-        for tokens in (FIRST, SECOND):
-            add_turned(turned[tokens.start], weighed(tokens), False, True)
-            sums[tokens.start] = turn_back(turned[tokens.start], "%d" % tokens.start)
-        last_terms[FIRST.start] = gated_term(1, FIRST)
-        for term, start in ((gated_term(3, late), True), (weighed(late), False)):
-            for tokens in (THIRD, FOURTH):
-                add_turned(turned[tokens.start], term[:, tokens.start - late.start : tokens.stop - late.start], start, False)
-        close(FIRST, sums[FIRST.start], last_terms[FIRST.start])
-        for tokens in (THIRD, FOURTH):
-            add_turned(turned[tokens.start], gated_term(2, tokens), False, True)
-            sums[tokens.start] = turn_back(turned[tokens.start], "%d" % tokens.start)
-        last_terms[SECOND.start] = gated_term(1, SECOND)
-        last_terms[THIRD.start] = gated_term(1, THIRD)
-        close(SECOND, sums[SECOND.start], last_terms[SECOND.start])
-        last_terms[FOURTH.start] = gated_term(1, FOURTH)
-        for tokens in (THIRD, FOURTH):
-            close(tokens, sums[tokens.start], last_terms[tokens.start])
+        def weigh_and_turn_back(number, turned, tokens):
+            for r in range(2):
+                for b in blocks_of(tokens):
+                    weight = gate_columns[:, r * blocks + b : r * blocks + b + 1]
+                    nc.scalar.activation(block(staged[r], b), block(turned[r], b - tokens.start // P), ACT.Copy, scale=weight)
+            sums = bank(number, [P, len(tokens)], "sums")
+            turn(sums, staged, tokens, True, True)
+            return sums
+
+        def close(sums, term, tokens):
+            nc.vector.tensor_tensor(columns(result, tokens), sums[:], term, ALU.add)
+            nc.sync.dma_start(columns(out, tokens), columns(result, tokens))
+
+        first, second = ONE_PLAIN
+        third, fourth = TWO_PLAIN
+        plain_term(0, first)
+        plain_term(0, second)
+        first_turned = three_turned(0, first)
+        second_turned = three_turned(1, second)
+        third_turned = [bank(2 + r, [P, len(third)], "turned") for r in range(2)]
+        two_turned(third_turned, third)
+        first_sums = turn_back(5, first_turned, first)
+        fourth_bank = bank(4, [P, 2, len(fourth)], "turned")
+        fourth_turned = [fourth_bank[:, r, :] for r in range(2)]
+        two_turned(fourth_turned, fourth)
+        second_sums = turn_back(6, second_turned, second)
+        third_sums = weigh_and_turn_back(7, third_turned, third)
+        fourth_sums = weigh_and_turn_back(0, fourth_turned, fourth)
+        first_term = gated_term(1, first, columns(terms[1], first))
+        third_terms = [gated_term(r, third, columns(terms[r], third)) for r in (3, 2)]
+        second_term = gated_term(1, second, columns(terms[1], second))
+        fourth_terms = [gated_term(2, fourth, columns(terms[2], fourth))]
+        nc.vector.tensor_tensor(third_terms[0], third_terms[0], third_terms[1], ALU.add)
+        close(first_sums, first_term, first)
+        fourth_terms.append(gated_term(3, fourth, columns(staged[0], first)))
+        close(second_sums, second_term, second)
+        fourth_pair = columns(staged[0], second)[:, : len(fourth)]
+        nc.vector.tensor_tensor(fourth_pair, fourth_terms[0], fourth_terms[1], ALU.add)
+        close(third_sums, third_terms[0], third)
+        close(fourth_sums, fourth_pair, fourth)

@@ -114,11 +114,11 @@ def tile_moe_ecr_mlp_relu2_kernel(
             return raw
 
         def quantize_w1(raw, count, vector_alone):
-            source = raw[:].rearrange("p o j (c v) -> p o c j v", v=4)
+            source = raw[:].rearrange("p o j (c v) -> p o c j v", v=2)
             half = H // 2
             rounded = [twos.tile([P, count, half, 4], BF16, name="w1_rounded%d" % u, align_bytes=64) for u in range(2)]
-            targets = [tile[:].rearrange("p o (c v) j -> p o c j v", v=4) for tile in rounded]
-            groups = half // 4
+            targets = [tile[:].rearrange("p o (c v) j -> p o c j v", v=2) for tile in rounded]
+            groups = half // 2
             nc.vector.tensor_copy(targets[0], source[:, :, :groups])
             if vector_alone:
                 nc.vector.tensor_copy(targets[1], source[:, :, groups:])
@@ -185,8 +185,8 @@ def tile_moe_ecr_mlp_relu2_kernel(
                 w2[experts[0] : experts[-1] + 1].rearrange("e (p j) n -> p e (j n)", j=4),
             )
             rounded = keep.tile([P, count, N, 4], BF16, name="w2_rounded", tag="w2_rounded%d" % experts[0], align_bytes=64)
-            target = rounded[:].rearrange("p e (c v) j -> p e c j v", v=4)
-            source = raw[:].rearrange("p e j (c v) -> p e c j v", v=4)
+            target = rounded[:].rearrange("p e (c v) j -> p e c j v", v=2)
+            source = raw[:].rearrange("p e j (c v) -> p e c j v", v=2)
             if on_scalar:
                 nc.scalar.copy(target, source)
             else:

@@ -119,7 +119,10 @@ def tile_moe_ecr_mlp_relu2_kernel(
             rounded = [twos.tile([P, count, half, 4], BF16, name="w1_rounded%d" % u, align_bytes=64) for u in range(2)]
             targets = [tile[:].rearrange("p o (c v) j -> p o c j v", v=2) for tile in rounded]
             groups = half // 2
-            nc.vector.tensor_copy(targets[0], source[:, :, :groups])
+            own = groups - groups // 8 if count == PASSES else groups
+            nc.vector.tensor_copy(targets[0][:, :, :own], source[:, :, :own])
+            if own < groups:
+                nc.scalar.copy(targets[0][:, :, own:], source[:, :, own:groups])
             if vector_alone:
                 nc.vector.tensor_copy(targets[1], source[:, :, groups:])
             else:

@@ -26,7 +26,8 @@ SHARED_FROM = 9
 EARLY_W2 = {5: (0, 1, 2, 3)}
 LATE_W2 = ((4,), (5, 6), (7,), (8,), (9, 10), (11,))
 LATE_ON_SCALAR = ((4,), (8,))
-VECTOR_ALONE = (10, 0)
+VECTOR_SIXTEENTHS = {(0, 0): 8, (0, 1): 8, (10, 0): 16, (10, 1): 8, (11, 0): 8, (11, 1): 8}
+WHOLE_SIXTEENTHS = 7
 LATE_Y = ((4, 5, 6, 7), (8, 9, 10), (11,))
 ONE_PLAIN = (range(0, 256), range(256, 640))
 TWO_PLAIN = (range(640, 1024), range(1024, 1280))
@@ -74,24 +75,18 @@ def tile_moe_ecr_mlp_relu2_kernel(
         ident = keep.tile([P, P], F32, name="ident")
         make_identity(nc, ident[:])
 
-        blocks = T // P
+        blocks = (T - TWO_PLAIN[0].start) // P
         gate_rows = keep.tile([P, P], F32, name="gate_rows")
         nc.vector.memset(gate_rows[:], 0.0)
-        for r in range(TOP):
-            nc.scalar.dma_start(gate_rows[r * blocks : (r + 1) * blocks, :], gate[r, 0].rearrange("(b t) -> b t", t=P))
+        for r in range(2):
+            row = gate[r, 0, TWO_PLAIN[0].start :]
+            for low, high in ((0, 4), (4, blocks)):
+                piece = row[low * P : high * P].rearrange("(b t) -> b t", t=P)
+                nc.scalar.dma_start(gate_rows[r * blocks + low : r * blocks + high, :], piece)
         gate_turned = next_bank("second", [P, P], "gate_turned")
         nc.tensor.transpose(gate_turned[:], gate_rows[:], ident[:])
-        gate_columns = keep.tile([P, TOP * blocks], F32, name="gate_columns")
-        nc.scalar.copy(gate_columns[:], gate_turned[:, : TOP * blocks])
-        spread_blocks = [(r, b) for r in range(TOP) for b in range(blocks) if r > 1 or b < TWO_PLAIN[0].start // P]
-        gates = keep.tile([P, len(spread_blocks) * P], F32, name="gates")
-        for first in range(0, len(spread_blocks), 4):
-            group = spread_blocks[first : first + 4]
-            spread = next_bank("first", [P, len(group), P], "gate_spread")
-            for place, (r, b) in enumerate(group):
-                column = gate_columns[:, r * blocks + b : r * blocks + b + 1]
-                nc.tensor.transpose(spread[:, place, :], column.to_broadcast([P, P]), ident[:])
-            nc.scalar.copy(gates[:, first * P : (first + len(group)) * P], spread[:].rearrange("p b t -> p (b t)"))
+        gate_columns = keep.tile([P, 2 * blocks], F32, name="gate_columns")
+        nc.scalar.copy(gate_columns[:], gate_turned[:, : 2 * blocks])
 
         slot_words, slot_scales = {}, {}
 
@@ -113,20 +108,20 @@ def tile_moe_ecr_mlp_relu2_kernel(
             )
             return raw
 
-        def quantize_w1(raw, count, vector_alone):
+        def quantize_w1(raw, count, sixteenths):
             source = raw[:].rearrange("p o j (c v) -> p o c j v", v=2)
             half = H // 2
             rounded = [twos.tile([P, count, half, 4], BF16, name="w1_rounded%d" % u, align_bytes=64) for u in range(2)]
             targets = [tile[:].rearrange("p o (c v) j -> p o c j v", v=2) for tile in rounded]
             groups = half // 2
-            own = groups - groups // 8 if count == PASSES else groups
-            nc.vector.tensor_copy(targets[0][:, :, :own], source[:, :, :own])
-            if own < groups:
-                nc.scalar.copy(targets[0][:, :, own:], source[:, :, own:groups])
-            if vector_alone:
-                nc.vector.tensor_copy(targets[1], source[:, :, groups:])
-            else:
-                nc.scalar.copy(targets[1], source[:, :, groups:])
+            cut = sixteenths * groups // 8
+            for u, target in enumerate(targets):
+                low, high = u * groups, (u + 1) * groups
+                middle = min(max(cut, low), high)
+                if middle > low:
+                    nc.vector.tensor_copy(target[:, :, : middle - low], source[:, :, low:middle])
+                if middle < high:
+                    nc.scalar.copy(target[:, :, middle - low :], source[:, :, middle:high])
             made = []
             for u, tile in enumerate(rounded):
                 codes = codes_ring.tile([P, count, half], U32, name="w1_codes%d" % u, align_bytes=64)
@@ -232,7 +227,7 @@ def tile_moe_ecr_mlp_relu2_kernel(
             count = 1 if e in BY_PASS else PASSES
             loaded = [load_w1(e, first, count) for first in range(0, PASSES, count)]
             w1_quantized = [
-                made for o, raw in enumerate(loaded) for made in quantize_w1(raw, count, (e, o) == VECTOR_ALONE)
+                made for o, raw in enumerate(loaded) for made in quantize_w1(raw, count, VECTOR_SIXTEENTHS.get((e, o), WHOLE_SIXTEENTHS))
             ]
             if 1 < e <= SHARED_FROM:
                 quantize_h(e - 2, square_h(turned[e - 2], loaded[0][:, count - 1, 2, H // 2 :]))
@@ -264,8 +259,19 @@ def tile_moe_ecr_mlp_relu2_kernel(
         for experts in LATE_Y:
             second_layer(experts)
 
-        terms = [raws.tile([P, T], F32, name="raw", tag="raw", align_bytes=64) for r in range(TOP)]
-        staged = [raws.tile([P, T], F32, name="raw", tag="raw", align_bytes=64) for r in range(2)]
+        terms = [raws.tile([P, T], F32, name="raw", tag="raw", align_bytes=64) for r in range(TOP - 1)]
+        half = TWO_PLAIN[0].start
+        gates_early = raws.tile([P, TOP, half], F32, name="raw", tag="raw", align_bytes=64)
+        for tokens in ONE_PLAIN:
+            for ranks in (slice(2, 4), slice(0, 2)):
+                nc.sync.dma_start(
+                    gates_early[:, ranks, tokens.start : tokens.stop],
+                    gate[ranks, :, tokens.start : tokens.stop].rearrange("r p t -> p r t"),
+                )
+        gates_late = raws.tile([P, 2, T - half], F32, name="raw", tag="raw", align_bytes=64)
+        nc.sync.dma_start(gates_late[:], gate[2:, :, half:].rearrange("r p t -> p r t"))
+        terms.append(raws.tile([P, T], F32, name="raw", tag="raw", align_bytes=64))
+        staged = [keep.tile([P, T], F32, name="staged%d" % r) for r in range(2)]
         result = keep.tile([P, T], F32, name="result")
 
         def picked(r, tokens):
@@ -281,8 +287,9 @@ def tile_moe_ecr_mlp_relu2_kernel(
             return range(tokens.start // P, tokens.stop // P)
 
         def gate_of(r, tokens):
-            first = spread_blocks.index((r, tokens.start // P)) * P
-            return gates[:, first : first + len(tokens)]
+            if tokens.start < half:
+                return gates_early[:, r, tokens.start : tokens.stop]
+            return gates_late[:, r - 2, tokens.start - half : tokens.stop - half]
 
         def turn(into, sources, tokens, start, stop):
             steps = [(source, b) for source in sources for b in blocks_of(tokens)]
@@ -326,7 +333,8 @@ def tile_moe_ecr_mlp_relu2_kernel(
         def weigh_and_turn_back(number, turned, tokens):
             for r in range(2):
                 for b in blocks_of(tokens):
-                    weight = gate_columns[:, r * blocks + b : r * blocks + b + 1]
+                    place = r * blocks + b - half // P
+                    weight = gate_columns[:, place : place + 1]
                     nc.scalar.activation(block(staged[r], b), block(turned[r], b - tokens.start // P), ACT.Copy, scale=weight)
             sums = bank(number, [P, len(tokens)], "sums")
             turn(sums, staged, tokens, True, True)

from contextlib import ExitStack

import concourse.mybir as mybir
from concourse.masks import make_identity

K, T, E, C, H, N = 1024, 1280, 12, 128, 512, 128
TOP, PAD = 4, 64
SLOTS = E * C
FLOPS = 2 * SLOTS * (K * H + H * N)

F32 = mybir.dt.float32
BF16 = mybir.dt.bfloat16
I32 = mybir.dt.int32
U32 = mybir.dt.uint32
U16 = mybir.dt.uint16
U8 = mybir.dt.uint8
FP8X4 = mybir.dt.float8_e4m3fn_x4
ALU = mybir.AluOpType
ACT = mybir.ActivationFunctionType

P = 128
PASSES = K // 512
PIECE = 256
BY_PASS = (0, 10, 11)
SHARED_FROM = 9
EARLY_W2 = {5: (0, 1, 2, 3)}
LATE_W2 = ((4,), (5, 6), (7,), (8,), (9, 10), (11,))
LATE_ON_SCALAR = ((4,), (8,))
VECTOR_SIXTEENTHS = {(0, 0): 8, (0, 1): 8, (10, 0): 16, (10, 1): 8, (11, 0): 8, (11, 1): 8}
WHOLE_SIXTEENTHS = 7
LATE_Y = ((4, 5, 6, 7), (8, 9, 10), (11,))
ONE_PLAIN = (range(0, 256), range(256, 640))
TWO_PLAIN = (range(640, 1024), range(1024, 1280))


def tile_moe_ecr_mlp_relu2_kernel(
    tc, x_words, x_scales, w1, w2, gate, offs, pos1, pos2, pos3, pos4, out
):
    nc = tc.nc
    with ExitStack() as ctx:
        lists = ctx.enter_context(tc.tile_pool(name="lists", bufs=1))
        keep = ctx.enter_context(tc.tile_pool(name="keep", bufs=1))
        raws = ctx.enter_context(tc.tile_pool(name="raws", bufs=7))
        codes_ring = ctx.enter_context(tc.tile_pool(name="codes_ring", bufs=4))
        twos = ctx.enter_context(tc.tile_pool(name="twos", bufs=2))
        psum = ctx.enter_context(tc.psum_pool(name="psum", bufs=1))
        turns = {"first": [], "second": []}

        def bank(number, shape, name):
            return psum.tile(shape, F32, name=name, tag="bank%d" % number)

        def next_bank(ring, shape, name):
            turns[ring].append(name)
            return bank((len(turns[ring]) - 1) % 4 + (4 if ring == "second" else 0), shape, name)


        token_scales = keep.tile([P, T], U8, name="token_scales", align_bytes=64)
        nc.vector.memset(token_scales[:].bitcast(I32), 0)
        y_all = keep.tile([P, SLOTS + PAD], F32, name="y_all")
        nc.vector.memset(y_all[:, SLOTS:], 0.0)

        token_words = []
        for o in range(PASSES):
            words = keep.tile([P, T], I32, name="token_words%d" % o, align_bytes=64)
            nc.sync.dma_start(words[:], x_words[o].rearrange("p t r -> p (t r)").bitcast(I32))
            token_words.append(words)
            if o == 0:
                offs_sb = lists.tile([P, SLOTS // 16], U16, name="offs_sb")
                nc.sync.dma_start(offs_sb[:], offs)
        for q in range(4):
            rows = slice(32 * q, 32 * q + 4 * PASSES)
            scale_rows = raws.tile([P, T // 4], I32, name="raw", tag="raw", align_bytes=64)
            nc.gpsimd.dma_start(scale_rows[rows, :], x_scales[:, 4 * q : 4 * q + 4, :].bitcast(I32))
            nc.vector.tensor_copy(token_scales[rows, :].bitcast(I32), scale_rows[rows, :])
        ident = keep.tile([P, P], F32, name="ident")
        make_identity(nc, ident[:])

        blocks = (T - TWO_PLAIN[0].start) // P
        gate_rows = keep.tile([P, P], F32, name="gate_rows")
        nc.vector.memset(gate_rows[:], 0.0)
        for r in range(2):
            row = gate[r, 0, TWO_PLAIN[0].start :]
            for low, high in ((0, 4), (4, blocks)):
                piece = row[low * P : high * P].rearrange("(b t) -> b t", t=P)
                nc.scalar.dma_start(gate_rows[r * blocks + low : r * blocks + high, :], piece)
        gate_turned = next_bank("second", [P, P], "gate_turned")
        nc.tensor.transpose(gate_turned[:], gate_rows[:], ident[:])
        gate_columns = keep.tile([P, 2 * blocks], F32, name="gate_columns")
        nc.scalar.copy(gate_columns[:], gate_turned[:, : 2 * blocks])

        slot_words, slot_scales = {}, {}

        def gather_tokens(piece):
            picks = offs_sb[:, piece * PIECE // 16 : (piece + 1) * PIECE // 16]
            for o in range(PASSES):
                words = twos.tile([P, PIECE], U32, name="slot_words%d" % o, align_bytes=64)
                nc.vector.tensor_copy(words[:], token_words[o][:].bitcast(U32).indirect(picks))
                slot_words[piece, o] = words
            scales = twos.tile([P, PIECE], U8, name="slot_scales", align_bytes=64)
            nc.vector.tensor_copy(scales[:], token_scales[:].indirect(picks))
            slot_scales[piece] = scales

        def load_w1(e, first, count):
            raw = raws.tile([P, count, 4, H], F32, name="raw", tag="raw", align_bytes=64)
            nc.sync.dma_start(
                raw[:].rearrange("p o j i -> p o (j i)"),
                w1[e, 512 * first : 512 * (first + count), :].rearrange("(o p j) i -> p o (j i)", p=P, j=4),
            )
            return raw

        def quantize_w1(raw, count, sixteenths):
            source = raw[:].rearrange("p o j (c v) -> p o c j v", v=2)
            half = H // 2
            rounded = [twos.tile([P, count, half, 4], BF16, name="w1_rounded%d" % u, align_bytes=64) for u in range(2)]
            targets = [tile[:].rearrange("p o (c v) j -> p o c j v", v=2) for tile in rounded]
            groups = half // 2
            cut = sixteenths * groups // 8
            for u, target in enumerate(targets):
                low, high = u * groups, (u + 1) * groups
                middle = min(max(cut, low), high)
                if middle > low:
                    nc.vector.tensor_copy(target[:, :, : middle - low], source[:, :, low:middle])
                if middle < high:
                    nc.scalar.copy(target[:, :, middle - low :], source[:, :, middle:high])
            made = []
            for u, tile in enumerate(rounded):
                codes = codes_ring.tile([P, count, half], U32, name="w1_codes%d" % u, align_bytes=64)
                scales = codes_ring.tile([P, count, half], U8, name="w1_scales%d" % u, align_bytes=64)
                nc.vector.quantize_mx(
                    out=codes[:].rearrange("p o i -> p (o i)").bitcast(FP8X4),
                    scales=scales[:].rearrange("p o i -> p (o i)"),
                    in_=tile[:].rearrange("p o i j -> p (o i j)"),
                )
                made.append((codes, scales))
            return [[(codes[:, o], scales[:, o]) for codes, scales in made] for o in range(count)]

        def first_product(e, w1_quantized):
            piece, first = divmod(e * C, PIECE)
            slots = slice(first, first + C)
            a = next_bank("first", [P, 2, H // 2], "a")
            for o in range(PASSES):
                for u in range(2):
                    codes, scales = w1_quantized[o][u]
                    nc.tensor.matmul_mx(
                        out=a[:, u, :],
                        lhsT=slot_words[piece, o][:, slots].bitcast(FP8X4),
                        lhsT_scale=slot_scales[piece][4 * o :, slots],
                        rhs=codes.bitcast(FP8X4),
                        rhs_scale=scales,
                        start=(o, u) == (0, 0),
                        stop=(o, u) == (PASSES - 1, 1),
                    )
            return a

        h_quantized = {}

        def turn_h(a, positive):
            nc.scalar.activation(positive, a[:].rearrange("s g (p j) -> s j (g p)", j=4), ACT.Relu)
            turned = next_bank("second", [P, 4, C], "h_turned")
            for j in range(4):
                nc.tensor.transpose(turned[:, j, :], positive[:, j, :], ident[:])
            return turned

        def square_h(turned, h):
            values = h.bitcast(BF16)
            nc.scalar.activation(values.rearrange("p (s j) -> p s j", j=4), turned[:].rearrange("p j s -> p s j"), ACT.Square)
            return values

        def quantize_h(e, values):
            room = "w2_rounded%d" % e if e == E - 1 else "h_codes%d" % e
            codes = keep.tile([P, C], U32, name="h_codes", tag=room, align_bytes=64)
            scales = keep.tile([P, C], U8, name="h_scales%d" % e, align_bytes=64)
            nc.vector.quantize_mx(out=codes[:].bitcast(FP8X4), scales=scales[:], in_=values)
            h_quantized[e] = (codes, scales)

        w2_quantized = {}

        def round_w2(experts, on_scalar):
            count = len(experts)
            raw = raws.tile([P, count, 4, N], F32, name="raw", tag="raw", align_bytes=64)
            nc.sync.dma_start(
                raw[:].rearrange("p e j n -> p e (j n)"),
                w2[experts[0] : experts[-1] + 1].rearrange("e (p j) n -> p e (j n)", j=4),
            )
            rounded = keep.tile([P, count, N, 4], BF16, name="w2_rounded", tag="w2_rounded%d" % experts[0], align_bytes=64)
            target = rounded[:].rearrange("p e (c v) j -> p e c j v", v=2)
            source = raw[:].rearrange("p e j (c v) -> p e c j v", v=2)
            if on_scalar:
                nc.scalar.copy(target, source)
            else:
                nc.vector.tensor_copy(target, source)
            return rounded

        def quantize_w2(experts, rounded):
            count = len(experts)
            codes = keep.tile([P, count, N], U32, name="w2_codes%d" % experts[0], align_bytes=64)
            scales = keep.tile([P, count, N], U8, name="w2_scales%d" % experts[0], align_bytes=64)
            nc.vector.quantize_mx(
                out=codes[:].rearrange("p e n -> p (e n)").bitcast(FP8X4),
                scales=scales[:].rearrange("p e n -> p (e n)"),
                in_=rounded[:].rearrange("p e n j -> p (e n j)"),
            )
            for place, e in enumerate(experts):
                w2_quantized[e] = (codes[:, place], scales[:, place])

        def second_layer(experts):
            y = next_bank("second", [P, len(experts) * C], "y")
            for place, e in enumerate(experts):
                codes, scales = w2_quantized[e]
                h_codes, h_scales = h_quantized[e]
                nc.tensor.matmul_mx(
                    out=y[:, place * C : (place + 1) * C],
                    lhsT=codes.bitcast(FP8X4),
                    lhsT_scale=scales,
                    rhs=h_codes[:].bitcast(FP8X4),
                    rhs_scale=h_scales[:],
                    start=True,
                    stop=True,
                )
            nc.scalar.copy(y_all[:, experts[0] * C : (experts[-1] + 1) * C], y[:])

        pos_sb = []
        products, turned = {}, {}
        for e in range(E):
            if e * C % PIECE == 0:
                gather_tokens(e * C // PIECE)
            count = 1 if e in BY_PASS else PASSES
            loaded = [load_w1(e, first, count) for first in range(0, PASSES, count)]
            w1_quantized = [
                made for o, raw in enumerate(loaded) for made in quantize_w1(raw, count, VECTOR_SIXTEENTHS.get((e, o), WHOLE_SIXTEENTHS))
            ]
            if 1 < e <= SHARED_FROM:
                quantize_h(e - 2, square_h(turned[e - 2], loaded[0][:, count - 1, 2, H // 2 :]))
            if e > 0:
                turned[e - 1] = turn_h(products[e - 1], loaded[0][:, 0, :, H - P :])
            if e > SHARED_FROM:
                for done in range(len(h_quantized), e):
                    words = twos.tile([P, H // 2], F32, name="h_words", align_bytes=64)
                    quantize_h(done, square_h(turned[done], words[:]))
            products[e] = first_product(e, w1_quantized)
            if e == 1:
                for r, pos in enumerate((pos1, pos2, pos3, pos4)):
                    tile = lists.tile([P, T // 16], U16, name="pos_sb%d" % r)
                    nc.sync.dma_start(tile[:], pos)
                    pos_sb.append(tile)
            if e in EARLY_W2:
                quantize_w2(EARLY_W2[e], round_w2(EARLY_W2[e], False))
                second_layer(EARLY_W2[e])
        last_h = keep.tile([P, H // 2], F32, name="last_h", align_bytes=64)
        last_positive = keep.tile([P, 4, P], F32, name="last_positive")
        last_values = square_h(turn_h(products[E - 1], last_positive[:]), last_h[:])
        waiting = []
        for experts in LATE_W2:
            waiting.append((experts, round_w2(experts, experts in LATE_ON_SCALAR)))
            if len(waiting) == 2:
                quantize_w2(*waiting.pop(0))
        quantize_w2(*waiting.pop(0))
        quantize_h(E - 1, last_values)
        for experts in LATE_Y:
            second_layer(experts)

        terms = [raws.tile([P, T], F32, name="raw", tag="raw", align_bytes=64) for r in range(TOP - 1)]
        half = TWO_PLAIN[0].start
        gates_early = raws.tile([P, TOP, half], F32, name="raw", tag="raw", align_bytes=64)
        for tokens in ONE_PLAIN:
            for ranks in (slice(2, 4), slice(0, 2)):
                nc.sync.dma_start(
                    gates_early[:, ranks, tokens.start : tokens.stop],
                    gate[ranks, :, tokens.start : tokens.stop].rearrange("r p t -> p r t"),
                )
        gates_late = raws.tile([P, 2, T - half], F32, name="raw", tag="raw", align_bytes=64)
        nc.sync.dma_start(gates_late[:], gate[2:, :, half:].rearrange("r p t -> p r t"))
        terms.append(raws.tile([P, T], F32, name="raw", tag="raw", align_bytes=64))
        staged = [keep.tile([P, T], F32, name="staged%d" % r) for r in range(2)]
        result = keep.tile([P, T], F32, name="result")

        def picked(r, tokens):
            return y_all[:].indirect(pos_sb[r][:, tokens.start // 16 : tokens.stop // 16])

        def columns(tile, tokens):
            return tile[:, tokens.start : tokens.stop]

        def block(tile, b):
            return tile[:, b * P : (b + 1) * P]

        def blocks_of(tokens):
            return range(tokens.start // P, tokens.stop // P)

        def gate_of(r, tokens):
            if tokens.start < half:
                return gates_early[:, r, tokens.start : tokens.stop]
            return gates_late[:, r - 2, tokens.start - half : tokens.stop - half]

        def turn(into, sources, tokens, start, stop):
            steps = [(source, b) for source in sources for b in blocks_of(tokens)]
            for step, (source, b) in enumerate(steps):
                nc.tensor.matmul(
                    block(into, b - tokens.start // P),
                    lhsT=block(source, b),
                    rhs=ident[:],
                    is_transpose=True,
                    start=start and step == 0,
                    stop=stop and step == len(steps) - 1,
                )

        def plain_term(r, tokens):
            nc.scalar.activation(columns(terms[r], tokens), picked(r, tokens), ACT.Copy)

        def gated_term(r, tokens, into):
            nc.vector.tensor_tensor(into, picked(r, tokens), gate_of(r, tokens), ALU.mult)
            return into

        def three_turned(number, tokens):
            turned = bank(number, [P, len(tokens)], "turned")
            for r in (3, 2):
                gated_term(r, tokens, columns(terms[r], tokens))
                turn(turned, [terms[r]], tokens, r == 3, False)
            nc.vector.tensor_tensor(columns(terms[0], tokens), columns(terms[0], tokens), gate_of(0, tokens), ALU.mult)
            turn(turned, [terms[0]], tokens, False, True)
            return turned

        def turn_back(number, turned, tokens):
            nc.scalar.copy(columns(staged[0], tokens), turned[:])
            sums = bank(number, [P, len(tokens)], "sums")
            turn(sums, staged[:1], tokens, True, True)
            return sums

        def two_turned(into, tokens):
            for r in range(2):
                plain_term(r, tokens)
                turn(into[r], [terms[r]], tokens, True, True)

        def weigh_and_turn_back(number, turned, tokens):
            for r in range(2):
                for b in blocks_of(tokens):
                    place = r * blocks + b - half // P
                    weight = gate_columns[:, place : place + 1]
                    nc.scalar.activation(block(staged[r], b), block(turned[r], b - tokens.start // P), ACT.Copy, scale=weight)
            sums = bank(number, [P, len(tokens)], "sums")
            turn(sums, staged, tokens, True, True)
            return sums

        def close(sums, term, tokens):
            nc.vector.tensor_tensor(columns(result, tokens), sums[:], term, ALU.add)
            nc.sync.dma_start(columns(out, tokens), columns(result, tokens))

        first, second = ONE_PLAIN
        third, fourth = TWO_PLAIN
        plain_term(0, first)
        plain_term(0, second)
        first_turned = three_turned(0, first)
        second_turned = three_turned(1, second)
        third_turned = [bank(2 + r, [P, len(third)], "turned") for r in range(2)]
        two_turned(third_turned, third)
        first_sums = turn_back(5, first_turned, first)
        fourth_bank = bank(4, [P, 2, len(fourth)], "turned")
        fourth_turned = [fourth_bank[:, r, :] for r in range(2)]
        two_turned(fourth_turned, fourth)
        second_sums = turn_back(6, second_turned, second)
        third_sums = weigh_and_turn_back(7, third_turned, third)
        fourth_sums = weigh_and_turn_back(0, fourth_turned, fourth)
        first_term = gated_term(1, first, columns(terms[1], first))
        third_terms = [gated_term(r, third, columns(terms[r], third)) for r in (3, 2)]
        second_term = gated_term(1, second, columns(terms[1], second))
        fourth_terms = [gated_term(2, fourth, columns(terms[2], fourth))]
        nc.vector.tensor_tensor(third_terms[0], third_terms[0], third_terms[1], ALU.add)
        close(first_sums, first_term, first)
        fourth_terms.append(gated_term(3, fourth, columns(staged[0], first)))
        close(second_sums, second_term, second)
        fourth_pair = columns(staged[0], second)[:, : len(fourth)]
        nc.vector.tensor_tensor(fourth_pair, fourth_terms[0], fourth_terms[1], ALU.add)
        close(third_sums, third_terms[0], third)
        close(fourth_sums, fourth_pair, fourth)
